import numpy as np
import ml_dtypes


def mxq(x, axis, fmt="e4m3"):
    dtype, down = {"e4m3": (ml_dtypes.float8_e4m3fn, 7), "e5m2": (ml_dtypes.float8_e5m2, 14)}[fmt]
    v = np.moveaxis(np.asarray(x, np.float32).astype(ml_dtypes.bfloat16).astype(np.float64), axis, -1)
    blocks = v.reshape(v.shape[:-1] + (-1, 32))
    amax = np.abs(blocks).max(-1, keepdims=True)
    byte = np.maximum(np.where(amax > 0, np.frexp(amax)[1] - 1 + 127, 0) - down, 1)
    scale = np.exp2(byte - 127.0)
    codes = (blocks / scale).astype(np.float32).astype(dtype).astype(np.float64)
    return np.moveaxis((codes * scale).reshape(v.shape), -1, axis)


WIDE = False


def mx_kscale(k):
    if not WIDE:
        return np.ones(k)
    levels = np.array([30, -30])
    if k % 512:
        return np.exp2(np.random.permutation(np.resize(levels, k // 32))).repeat(32)
    a = np.empty((k // 512, 16))
    for p in range(k // 512):
        a[p, :8] = np.random.permutation(np.resize(levels, 8))
        for g in range(8):
            far = levels[np.abs(levels - a[p, g]) >= 10]
            a[p, g + 8] = far[np.random.randint(len(far))]
    return np.exp2(a.ravel()).repeat(32)


def f64(x):
    return np.asarray(x).astype(np.float64)


E2M1 = np.array([0.0, 0.5, 1.0, 1.5, 2.0, 3.0, 4.0, 6.0, -0.0, -0.5, -1.0, -1.5, -2.0, -3.0, -4.0, -6.0])


def pack_weight(w, fmt):
    k, n = w.shape
    w = f64(np.asarray(w, np.float32).astype(ml_dtypes.bfloat16)).reshape(k // 32, 32, n)
    amax = np.abs(w).max(1)
    if fmt == "e4m3":
        byte = np.frexp(amax)[1] - 1 + 127 - 7
    else:
        mant, ex = np.frexp(amax / 6.0)
        byte = np.where(mant > 0.5, ex, ex - 1) + 127
    byte = np.clip(np.where(amax > 0, byte, 1), 1, 254)
    scaled = (w * np.exp2(127.0 - byte)[:, None, :]).reshape(k, n).astype(np.float32)
    by_word = np.ascontiguousarray(scaled.reshape(k // 512, 128, 4, n).transpose(0, 1, 3, 2))
    if fmt == "e4m3":
        words = by_word.astype(ml_dtypes.float8_e4m3fn).view(np.uint8)
    else:
        c = by_word.astype(ml_dtypes.float4_e2m1fn).view(np.uint8) & 0xF
        words = (c[..., 0::2] | (c[..., 1::2] << 4)).reshape(k // 512, 128, 2 * n)
    return np.ascontiguousarray(words), np.ascontiguousarray(byte.astype(np.uint8).reshape(k // 512, 16, n))


def unpack_weight(words, scales, fmt):
    g, _, n = scales.shape
    words = np.ascontiguousarray(words).reshape(g, 128, n, -1)
    if fmt == "e4m3":
        vals = words.view(ml_dtypes.float8_e4m3fn).astype(np.float64)
    else:
        nib = np.empty((g, 128, n, 4), np.uint8)
        nib[..., 0::2] = words & 0xF
        nib[..., 1::2] = words >> 4
        vals = E2M1[nib]
    vals = vals * np.repeat(np.exp2(scales.astype(np.float64) - 127.0), 8, axis=1)[..., None]
    return vals.transpose(0, 1, 3, 2).reshape(g * 512, n)


K, L, M, N = 512, 1024, 512, 1024


def setup_inputs():
    n = np.random.standard_normal
    s = mx_kscale(K)[:, None]
    u = mx_kscale(L)[:, None]
    bm = n((L, N)) / np.sqrt(L) / u
    b4 = pack_weight(bm, "e2m1")
    rest = bm - unpack_weight(*b4, "e2m1")
    p_b8 = pack_weight(rest, "e4m3")
    return {
        "g": (n((K, L)) / np.sqrt(K) * s * u.T).astype(np.float32),
        "am": (n((K, M)) / s).astype(np.float32),
        "b4_words": b4[0],
        "b4_scales": b4[1],
        "b8_words": p_b8[0],
        "b8_scales": p_b8[1],
    }


def reference(g, am, b4_words, b4_scales, b8_words, b8_scales):
    g_ = mxq(f64(g), 0, "e5m2")
    am_ = mxq(f64(am), 0, "e4m3")
    h = g_.T @ am_
    h_ = mxq(h, 0, "e4m3")
    b4_ = unpack_weight(b4_words, b4_scales, "e2m1")
    b8_ = unpack_weight(b8_words, b8_scales, "e4m3")
    y = h_.T @ b4_ + h_.T @ b8_
    return y

@@ -1,0 +1,236 @@
+from contextlib import ExitStack
+
+import concourse.mybir as mybir
+
+K, L, M, N = 512, 1024, 512, 1024
+FLOPS = 2 * K * L * M + 2 * 2 * L * M * N
+
+F32 = mybir.dt.float32
+BF16 = mybir.dt.bfloat16
+I32 = mybir.dt.int32
+U32 = mybir.dt.uint32
+U8 = mybir.dt.uint8
+E4M3 = mybir.dt.float8_e4m3fn_x4
+E5M2 = mybir.dt.float8_e5m2_x4
+E2M1 = mybir.dt.float4_e2m1fn_x4
+
+P = 128
+PACK = 4
+PASS = P * PACK
+BANK = 512
+CHUNK = 256
+CHUNK_P = CHUNK // PACK
+AM_V = 344
+G_V = {(0, 0): 24, (0, 1): 44, (1, 0): 64, (1, 1): 44}
+
+
+def tile_mix_kfac_res_none_kernel(tc, g, am, b4_words, b4_scales, b8_words, b8_scales, out):
+    nc = tc.nc
+    with ExitStack() as ctx:
+        sb = ctx.enter_context(tc.tile_pool(name="sb", bufs=1))
+        ys = ctx.enter_context(tc.tile_pool(name="ys", bufs=4))
+        ps = ctx.enter_context(tc.psum_pool(name="ps", bufs=1))
+        ctx.enter_context(tc.manual_schedule())
+
+        def keep(name, shape, dtype):
+            return sb.tile(shape, dtype, name=name, align_bytes=64)
+
+        def bank(n, name):
+            return ps.tile([P, BANK], F32, name=name, tag="bank%d" % n)
+
+        am_raw = keep("am_raw", [P, PACK, M], F32)
+        am_bf = keep("am_bf", [P, M, PACK], BF16)
+        am_codes = keep("am_codes", [P, M], U32)
+        am_scale = keep("am_scale", [P, M], U8)
+        g_raw = {(a, c): keep("g_raw%d%d" % (a, c), [P, PACK, CHUNK], F32) for a in range(2) for c in range(2)}
+        g_bf = [keep("g_bf%d" % a, [P, PACK, P, PACK], BF16) for a in range(2)]
+        g_codes = [keep("g_codes%d" % a, [P, PACK, P], U32) for a in range(2)]
+        g_scale = [keep("g_scale%d" % a, [P, PACK, P], U8) for a in range(2)]
+        h_rows = [keep("h_rows%d" % a, [P, PACK, M], BF16) for a in range(2)]
+        h_bf = {(a, t): keep("h_bf%d%d" % (a, t), [P, P, PACK], BF16) for a in range(2) for t in range(4)}
+        h_codes = {(a, t): keep("h_codes%d%d" % (a, t), [P, P], U32) for a in range(2) for t in range(4)}
+        h_scale = {(a, t): keep("h_scale%d%d" % (a, t), [P, P], U8) for a in range(2) for t in range(4)}
+        b4 = [keep("b4_%d" % a, [P, 2 * N], U8) for a in range(2)]
+        b8 = [keep("b8_%d" % a, [P, 4 * N], U8) for a in range(2)]
+        b4_plane = keep("b4_plane", [P, 2, N], U8)
+        b8_plane = keep("b8_plane", [P, N], U8)
+
+        g_k = g.rearrange("(p j) l -> p j l", j=PACK)
+
+        def load_g(a, c):
+            l0 = a * PASS + c * CHUNK
+            nc.sync.dma_start(out=g_raw[a, c][:], in_=g_k[:, :, l0 : l0 + CHUNK])
+
+        def load_b4_scales(q):
+            nc.sync.dma_start(
+                out=b4_plane[32 * q : 32 * q + 4, :, :].bitcast(I32),
+                in_=b4_scales[:, 4 * q : 4 * q + 4, :].rearrange("a r n -> r a n").bitcast(I32),
+            )
+
+        def load_b8_scales(q):
+            nc.sync.dma_start(
+                out=b8_plane[32 * q + 4 : 32 * q + 12, :].bitcast(I32),
+                in_=b8_scales[:, 4 * q : 4 * q + 4, :].bitcast(I32),
+            )
+
+        def load_b(a):
+            nc.sync.dma_start(out=b4[a][:].bitcast(I32), in_=b4_words[a].bitcast(I32))
+            nc.sync.dma_start(out=b8[a][:].bitcast(I32), in_=b8_words[a].rearrange("p n i -> p (n i)").bitcast(I32))
+
+        nc.vector.memset(b8_plane[:].bitcast(I32), 0)
+        nc.vector.memset(b4_plane[:].rearrange("p a n -> p (a n)").bitcast(I32), 0)
+        nc.sync.dma_start(out=am_raw[:], in_=am.rearrange("(p j) m -> p j m", j=PACK))
+        load_g(0, 0)
+        load_g(0, 1)
+        for q in range(4):
+            load_b8_scales(q)
+        load_g(1, 0)
+        load_g(1, 1)
+        for q in range(4):
+            load_b4_scales(q)
+        load_b(0)
+        load_b(1)
+
+        def copy_on(engine, dst, src):
+            if engine == "v":
+                nc.vector.tensor_copy(out=dst, in_=src)
+            else:
+                nc.scalar.copy(out=dst, in_=src)
+
+        def round_am(engine, m0, m1):
+            copy_on(
+                engine,
+                am_bf[:, m0:m1, :].rearrange("p (c u) j -> p c j u", u=4),
+                am_raw[:, :, m0:m1].rearrange("p j (c u) -> p c j u", u=4),
+            )
+
+        def round_g(engine, a, c, p0, p1):
+            copy_on(
+                engine,
+                g_bf[a][:, :, c * CHUNK_P + p0 : c * CHUNK_P + p1, :].rearrange("p i s j -> p s j i"),
+                g_raw[a, c][:, :, PACK * p0 : PACK * p1].rearrange("p j (s i) -> p s j i", i=PACK),
+            )
+
+        def round_g_chunk(a, c):
+            split = G_V[a, c]
+            round_g("v", a, c, 0, split)
+            if split < CHUNK_P:
+                round_g("s", a, c, split, CHUNK_P)
+
+        def quantize_g(a, i):
+            nc.vector.quantize_mx(
+                out=g_codes[a][:, i, :].bitcast(E5M2),
+                scales=g_scale[a][:, i, :],
+                in_=g_bf[a][:, i, :, :].rearrange("p s j -> p (s j)"),
+            )
+
+        h_banks = {}
+
+        def h_pass(a, i):
+            h_banks[a, i] = bank(4 * a + i, "h%d%d" % (a, i))
+            nc.tensor.matmul_mx(
+                out=h_banks[a, i][:],
+                lhsT=g_codes[a][:, i, :].bitcast(E5M2),
+                lhsT_scale=g_scale[a][:, i, :],
+                rhs=am_codes[:].bitcast(E4M3),
+                rhs_scale=am_scale[:],
+                start=True,
+                stop=True,
+            )
+
+        def drain_h(engine, a, i):
+            copy_on(engine, h_rows[a][:, i, :], h_banks[a, i][:])
+
+        def weave_h(engine, a, t):
+            copy_on(
+                engine,
+                h_bf[a, t][:].rearrange("p (c u) i -> p c i u", u=4),
+                h_rows[a][:, :, t * P : (t + 1) * P].rearrange("p i (c u) -> p c i u", u=4),
+            )
+
+        def quantize_h(a, t):
+            nc.vector.quantize_mx(
+                out=h_codes[a, t][:].bitcast(E4M3),
+                scales=h_scale[a, t][:],
+                in_=h_bf[a, t][:].rearrange("p m i -> p (m i)"),
+            )
+
+        y_banks = {}
+
+        def y_passes(a, t, half):
+            if a == 0:
+                y_banks[t, half] = bank(2 * t + half, "y%d%d" % (t, half))
+            n0 = half * BANK
+            nc.tensor.matmul_mx(
+                out=y_banks[t, half][:],
+                lhsT=h_codes[a, t][:].bitcast(E4M3),
+                lhsT_scale=h_scale[a, t][:],
+                rhs=b4[a][:, 2 * n0 : 2 * (n0 + BANK)].bitcast(E2M1),
+                rhs_scale=b4_plane[:, a, n0 : n0 + BANK],
+                start=(a == 0),
+                stop=False,
+            )
+            nc.tensor.matmul_mx(
+                out=y_banks[t, half][:],
+                lhsT=h_codes[a, t][:].bitcast(E4M3),
+                lhsT_scale=h_scale[a, t][:],
+                rhs=b8[a][:, 4 * n0 : 4 * (n0 + BANK)].bitcast(E4M3),
+                rhs_scale=b8_plane[4 + 4 * a :, n0 : n0 + BANK],
+                start=False,
+                stop=(a == 1),
+            )
+
+        def store_y(engine, t, half, pieces):
+            width = BANK // pieces
+            for piece in range(pieces):
+                y = ys.tile([P, width], F32, name="y", tag="y")
+                c0 = piece * width
+                copy_on(engine, y[:], y_banks[t, half][:, c0 : c0 + width])
+                n0 = half * BANK + c0
+                nc.sync.dma_start(out=out[t * P : (t + 1) * P, n0 : n0 + width], in_=y[:])
+
+        round_am("v", 0, AM_V)
+        round_am("s", AM_V, M)
+        nc.vector.quantize_mx(out=am_codes[:].bitcast(E4M3), scales=am_scale[:], in_=am_bf[:].rearrange("p m j -> p (m j)"))
+        round_g_chunk(0, 0)
+        round_g_chunk(0, 1)
+        for i in range(4):
+            quantize_g(0, i)
+            h_pass(0, i)
+        round_g_chunk(1, 0)
+        drain_h("s", 0, 0)
+        drain_h("s", 0, 1)
+        drain_h("v", 0, 2)
+        round_g_chunk(1, 1)
+        drain_h("s", 0, 3)
+        for i in range(4):
+            quantize_g(1, i)
+            h_pass(1, i)
+        for t in range(2):
+            weave_h("v", 0, t)
+            quantize_h(0, t)
+        for i in range(4):
+            drain_h("s", 1, i)
+        for t in range(2):
+            for half in range(2):
+                y_passes(0, t, half)
+        weave_h("v", 0, 2)
+        for t in range(2):
+            weave_h("v", 1, t)
+            quantize_h(1, t)
+        for t in range(2):
+            for half in range(2):
+                y_passes(1, t, half)
+                store_y("s", t, half, 1)
+        weave_h("v", 1, 2)
+        quantize_h(0, 2)
+        quantize_h(1, 2)
+        weave_h("v", 0, 3)
+        weave_h("v", 1, 3)
+        quantize_h(0, 3)
+        quantize_h(1, 3)
+        for t in range(2, 4):
+            for half in range(2):
+                y_passes(0, t, half)
+                y_passes(1, t, half)
+                store_y("s" if half == 0 else "v", t, half, 2 if (t, half) == (3, 1) else 1)

@@ -18,17 +18,19 @@ P = 128
 PACK = 4
 PASS = P * PACK
 BANK = 512
-CHUNK = 256
-CHUNK_P = CHUNK // PACK
-AM_V = 344
-G_V = {(0, 0): 24, (0, 1): 44, (1, 0): 64, (1, 1): 44}
+AM_CHUNK = 256
+AM_V = 168
+G_CHUNKS = {(0, 0): (0, 64), (0, 1): (64, 128), (1, 0): (0, 64), (1, 1): (64, 128)}
+G_V = {(0, 0): 42, (0, 1): 42, (1, 0): 14, (1, 1): 64}
+WARM = ((256, 4), (512, 3))
+TAIL = ((0, 256, 7, "s"), (256, 128, 0, "v"), (384, 128, 1, "s"))
 
 
 def tile_mix_kfac_res_none_kernel(tc, g, am, b4_words, b4_scales, b8_words, b8_scales, out):
     nc = tc.nc
     with ExitStack() as ctx:
         sb = ctx.enter_context(tc.tile_pool(name="sb", bufs=1))
-        ys = ctx.enter_context(tc.tile_pool(name="ys", bufs=4))
+        ys = ctx.enter_context(tc.tile_pool(name="ys", bufs=10))
         ps = ctx.enter_context(tc.psum_pool(name="ps", bufs=1))
         ctx.enter_context(tc.manual_schedule())
 
@@ -38,11 +40,11 @@ def tile_mix_kfac_res_none_kernel(tc, g, am, b4_words, b4_scales, b8_words, b8_s
         def bank(n, name):
             return ps.tile([P, BANK], F32, name=name, tag="bank%d" % n)
 
-        am_raw = keep("am_raw", [P, PACK, M], F32)
+        am_raw = [keep("am_raw%d" % c, [P, PACK, AM_CHUNK], F32) for c in range(2)]
         am_bf = keep("am_bf", [P, M, PACK], BF16)
         am_codes = keep("am_codes", [P, M], U32)
         am_scale = keep("am_scale", [P, M], U8)
-        g_raw = {(a, c): keep("g_raw%d%d" % (a, c), [P, PACK, CHUNK], F32) for a in range(2) for c in range(2)}
+        g_raw = {key: keep("g_raw%d%d" % key, [P, PACK, PACK * (s1 - s0)], F32) for key, (s0, s1) in G_CHUNKS.items()}
         g_bf = [keep("g_bf%d" % a, [P, PACK, P, PACK], BF16) for a in range(2)]
         g_codes = [keep("g_codes%d" % a, [P, PACK, P], U32) for a in range(2)]
         g_scale = [keep("g_scale%d" % a, [P, PACK, P], U8) for a in range(2)]
@@ -58,8 +60,8 @@ def tile_mix_kfac_res_none_kernel(tc, g, am, b4_words, b4_scales, b8_words, b8_s
         g_k = g.rearrange("(p j) l -> p j l", j=PACK)
 
         def load_g(a, c):
-            l0 = a * PASS + c * CHUNK
-            nc.sync.dma_start(out=g_raw[a, c][:], in_=g_k[:, :, l0 : l0 + CHUNK])
+            s0, s1 = G_CHUNKS[a, c]
+            nc.sync.dma_start(out=g_raw[a, c][:], in_=g_k[:, :, a * PASS + PACK * s0 : a * PASS + PACK * s1])
 
         def load_b4_scales(q):
             nc.sync.dma_start(
@@ -73,23 +75,31 @@ def tile_mix_kfac_res_none_kernel(tc, g, am, b4_words, b4_scales, b8_words, b8_s
                 in_=b8_scales[:, 4 * q : 4 * q + 4, :].bitcast(I32),
             )
 
-        def load_b(a):
+        def load_b4(a):
             nc.sync.dma_start(out=b4[a][:].bitcast(I32), in_=b4_words[a].bitcast(I32))
+
+        def load_b8(a):
             nc.sync.dma_start(out=b8[a][:].bitcast(I32), in_=b8_words[a].rearrange("p n i -> p (n i)").bitcast(I32))
 
         nc.vector.memset(b8_plane[:].bitcast(I32), 0)
         nc.vector.memset(b4_plane[:].rearrange("p a n -> p (a n)").bitcast(I32), 0)
-        nc.sync.dma_start(out=am_raw[:], in_=am.rearrange("(p j) m -> p j m", j=PACK))
+        am_k = am.rearrange("(p j) m -> p j m", j=PACK)
+        for c in range(2):
+            nc.sync.dma_start(out=am_raw[c][:], in_=am_k[:, :, c * AM_CHUNK : (c + 1) * AM_CHUNK])
         load_g(0, 0)
         load_g(0, 1)
-        for q in range(4):
-            load_b8_scales(q)
         load_g(1, 0)
         load_g(1, 1)
         for q in range(4):
             load_b4_scales(q)
-        load_b(0)
-        load_b(1)
+        load_b4(0)
+        load_b8_scales(0)
+        load_b8_scales(1)
+        load_b8(0)
+        load_b8_scales(2)
+        load_b8_scales(3)
+        load_b4(1)
+        load_b8(1)
 
         def copy_on(engine, dst, src):
             if engine == "v":
@@ -97,25 +107,34 @@ def tile_mix_kfac_res_none_kernel(tc, g, am, b4_words, b4_scales, b8_words, b8_s
             else:
                 nc.scalar.copy(out=dst, in_=src)
 
-        def round_am(engine, m0, m1):
+        def round_am(engine, c, m0, m1):
             copy_on(
                 engine,
-                am_bf[:, m0:m1, :].rearrange("p (c u) j -> p c j u", u=4),
-                am_raw[:, :, m0:m1].rearrange("p j (c u) -> p c j u", u=4),
+                am_bf[:, c * AM_CHUNK + m0 : c * AM_CHUNK + m1, :].rearrange("p (c u) j -> p c j u", u=4),
+                am_raw[c][:, :, m0:m1].rearrange("p j (c u) -> p c j u", u=4),
+            )
+
+        def quantize_am(c):
+            cols = slice(c * AM_CHUNK, (c + 1) * AM_CHUNK)
+            nc.vector.quantize_mx(
+                out=am_codes[:, cols].bitcast(E4M3),
+                scales=am_scale[:, cols],
+                in_=am_bf[:, cols, :].rearrange("p m j -> p (m j)"),
             )
 
         def round_g(engine, a, c, p0, p1):
             copy_on(
                 engine,
-                g_bf[a][:, :, c * CHUNK_P + p0 : c * CHUNK_P + p1, :].rearrange("p i s j -> p s j i"),
+                g_bf[a][:, :, G_CHUNKS[a, c][0] + p0 : G_CHUNKS[a, c][0] + p1, :].rearrange("p i s j -> p s j i"),
                 g_raw[a, c][:, :, PACK * p0 : PACK * p1].rearrange("p j (s i) -> p s j i", i=PACK),
             )
 
         def round_g_chunk(a, c):
             split = G_V[a, c]
             round_g("v", a, c, 0, split)
-            if split < CHUNK_P:
-                round_g("s", a, c, split, CHUNK_P)
+            width = G_CHUNKS[a, c][1] - G_CHUNKS[a, c][0]
+            if split < width:
+                round_g("s", a, c, split, width)
 
         def quantize_g(a, i):
             nc.vector.quantize_mx(
@@ -138,8 +157,8 @@ def tile_mix_kfac_res_none_kernel(tc, g, am, b4_words, b4_scales, b8_words, b8_s
                 stop=True,
             )
 
-        def drain_h(engine, a, i):
-            copy_on(engine, h_rows[a][:, i, :], h_banks[a, i][:])
+        def drain_h(engine, a, i, m0=0, m1=M):
+            copy_on(engine, h_rows[a][:, i, m0:m1], h_banks[a, i][:, m0:m1])
 
         def weave_h(engine, a, t):
             copy_on(
@@ -157,80 +176,107 @@ def tile_mix_kfac_res_none_kernel(tc, g, am, b4_words, b4_scales, b8_words, b8_s
 
         y_banks = {}
 
-        def y_passes(a, t, half):
-            if a == 0:
+        def b4_pass(acc, a, t, n0, width, start, stop):
+            nc.tensor.matmul_mx(
+                out=acc,
+                lhsT=h_codes[a, t][:].bitcast(E4M3),
+                lhsT_scale=h_scale[a, t][:],
+                rhs=b4[a][:, 2 * n0 : 2 * (n0 + width)].bitcast(E2M1),
+                rhs_scale=b4_plane[:, a, n0 : n0 + width],
+                start=start,
+                stop=stop,
+            )
+
+        def b8_pass(acc, a, t, n0, width, start, stop):
+            nc.tensor.matmul_mx(
+                out=acc,
+                lhsT=h_codes[a, t][:].bitcast(E4M3),
+                lhsT_scale=h_scale[a, t][:],
+                rhs=b8[a][:, 4 * n0 : 4 * (n0 + width)].bitcast(E4M3),
+                rhs_scale=b8_plane[4 + 4 * a :, n0 : n0 + width],
+                start=start,
+                stop=stop,
+            )
+
+        def open_y(t):
+            for half in range(2):
                 y_banks[t, half] = bank(2 * t + half, "y%d%d" % (t, half))
-            n0 = half * BANK
-            nc.tensor.matmul_mx(
-                out=y_banks[t, half][:],
-                lhsT=h_codes[a, t][:].bitcast(E4M3),
-                lhsT_scale=h_scale[a, t][:],
-                rhs=b4[a][:, 2 * n0 : 2 * (n0 + BANK)].bitcast(E2M1),
-                rhs_scale=b4_plane[:, a, n0 : n0 + BANK],
-                start=(a == 0),
-                stop=False,
-            )
-            nc.tensor.matmul_mx(
-                out=y_banks[t, half][:],
-                lhsT=h_codes[a, t][:].bitcast(E4M3),
-                lhsT_scale=h_scale[a, t][:],
-                rhs=b8[a][:, 4 * n0 : 4 * (n0 + BANK)].bitcast(E4M3),
-                rhs_scale=b8_plane[4 + 4 * a :, n0 : n0 + BANK],
-                start=False,
-                stop=(a == 1),
-            )
+                b4_pass(y_banks[t, half][:], 0, t, half * BANK, BANK, True, False)
+            for half in range(2):
+                b8_pass(y_banks[t, half][:], 0, t, half * BANK, BANK, False, False)
 
-        def store_y(engine, t, half, pieces):
-            width = BANK // pieces
-            for piece in range(pieces):
-                y = ys.tile([P, width], F32, name="y", tag="y")
-                c0 = piece * width
-                copy_on(engine, y[:], y_banks[t, half][:, c0 : c0 + width])
-                n0 = half * BANK + c0
-                nc.sync.dma_start(out=out[t * P : (t + 1) * P, n0 : n0 + width], in_=y[:])
+        def store_y(engine, acc, t, n0, width):
+            y = ys.tile([P, width], F32, name="y", tag="y")
+            copy_on(engine, y[:], acc)
+            nc.sync.dma_start(out=out[t * P : (t + 1) * P, n0 : n0 + width], in_=y[:])
 
-        round_am("v", 0, AM_V)
-        round_am("s", AM_V, M)
-        nc.vector.quantize_mx(out=am_codes[:].bitcast(E4M3), scales=am_scale[:], in_=am_bf[:].rearrange("p m j -> p (m j)"))
+        def close_y(engine, t, half):
+            b4_pass(y_banks[t, half][:], 1, t, half * BANK, BANK, False, False)
+            b8_pass(y_banks[t, half][:], 1, t, half * BANK, BANK, False, True)
+            store_y(engine, y_banks[t, half][:], t, half * BANK, BANK)
+
+        def whole_y(engine, number, t, n0, width):
+            acc = bank(number, "y%d_%d" % (t, n0))
+            step = BANK if width == BANK else P
+            b8_pass(acc[:, :width], 0, t, n0, width, True, False)
+            for a in range(2):
+                for c0 in range(0, width, step):
+                    b4_pass(acc[:, c0 : c0 + step], a, t, n0 + c0, step, False, False)
+            b8_pass(acc[:, :width], 1, t, n0, width, False, True)
+            store_y(engine, acc[:, :width], t, n0, width)
+
+        warm = bank(7, "warm")
+        for c in range(2):
+            round_am("v", c, 0, AM_V)
+            round_am("s", c, AM_V, AM_CHUNK)
+            quantize_am(c)
+            width, count = WARM[c]
+            for w in range(count):
+                nc.tensor.matmul_mx(
+                    out=warm[:, :width],
+                    lhsT=am_codes[:, :P].bitcast(E4M3),
+                    lhsT_scale=am_scale[:, :P],
+                    rhs=am_codes[:, :width].bitcast(E4M3),
+                    rhs_scale=am_scale[:, :width],
+                    start=True,
+                    stop=True,
+                )
         round_g_chunk(0, 0)
         round_g_chunk(0, 1)
         for i in range(4):
             quantize_g(0, i)
             h_pass(0, i)
         round_g_chunk(1, 0)
-        drain_h("s", 0, 0)
-        drain_h("s", 0, 1)
-        drain_h("v", 0, 2)
         round_g_chunk(1, 1)
-        drain_h("s", 0, 3)
+        for m0 in (0, 2 * P):
+            for i in range(4):
+                drain_h("s", 0, i, m0, m0 + 2 * P)
         for i in range(4):
             quantize_g(1, i)
             h_pass(1, i)
         for t in range(2):
             weave_h("v", 0, t)
             quantize_h(0, t)
-        for i in range(4):
+            open_y(t)
+        for i in range(3):
             drain_h("s", 1, i)
-        for t in range(2):
-            for half in range(2):
-                y_passes(0, t, half)
         weave_h("v", 0, 2)
-        for t in range(2):
-            weave_h("v", 1, t)
-            quantize_h(1, t)
-        for t in range(2):
-            for half in range(2):
-                y_passes(1, t, half)
-                store_y("s", t, half, 1)
-        weave_h("v", 1, 2)
+        drain_h("v", 1, 3)
         quantize_h(0, 2)
-        quantize_h(1, 2)
+        open_y(2)
+        weave_h("v", 1, 0)
+        weave_h("v", 1, 1)
+        quantize_h(1, 0)
+        quantize_h(1, 1)
+        weave_h("v", 1, 2)
         weave_h("v", 0, 3)
+        quantize_h(1, 2)
         weave_h("v", 1, 3)
         quantize_h(0, 3)
         quantize_h(1, 3)
-        for t in range(2, 4):
+        for t in range(3):
             for half in range(2):
-                y_passes(0, t, half)
-                y_passes(1, t, half)
-                store_y("s" if half == 0 else "v", t, half, 2 if (t, half) == (3, 1) else 1)
+                close_y("s" if (t, half) != (2, 0) else "v", t, half)
+        whole_y("s", 6, 3, 0, BANK)
+        for c0, width, number, engine in TAIL:
+            whole_y(engine, number, 3, BANK + c0, width)

@@ -21,7 +21,7 @@ BANK = 512
 AM_CHUNK = 256
 AM_V = 168
 G_CHUNKS = {(0, 0): (0, 64), (0, 1): (64, 128), (1, 0): (0, 64), (1, 1): (64, 128)}
-G_V = {(0, 0): 42, (0, 1): 42, (1, 0): 14, (1, 1): 64}
+G_V = {(0, 0): 44, (0, 1): 44, (1, 0): 64, (1, 1): 64}
 WARM = ((256, 4), (512, 3))
 TAIL = ((0, 256, 7, "s"), (256, 128, 0, "v"), (384, 128, 1, "s"))
 
@@ -70,7 +70,7 @@ def tile_mix_kfac_res_none_kernel(tc, g, am, b4_words, b4_scales, b8_words, b8_s
             )
 
         def load_b8_scales(q):
-            nc.sync.dma_start(
+            nc.gpsimd.dma_start(
                 out=b8_plane[32 * q + 4 : 32 * q + 12, :].bitcast(I32),
                 in_=b8_scales[:, 4 * q : 4 * q + 4, :].bitcast(I32),
             )
@@ -81,7 +81,9 @@ def tile_mix_kfac_res_none_kernel(tc, g, am, b4_words, b4_scales, b8_words, b8_s
         def load_b8(a):
             nc.sync.dma_start(out=b8[a][:].bitcast(I32), in_=b8_words[a].rearrange("p n i -> p (n i)").bitcast(I32))
 
-        nc.vector.memset(b8_plane[:].bitcast(I32), 0)
+        nc.gpsimd.memset(b8_plane[:].bitcast(I32), 0)
+        for q in range(4):
+            load_b8_scales(q)
         nc.vector.memset(b4_plane[:].rearrange("p a n -> p (a n)").bitcast(I32), 0)
         am_k = am.rearrange("(p j) m -> p j m", j=PACK)
         for c in range(2):
@@ -93,11 +95,7 @@ def tile_mix_kfac_res_none_kernel(tc, g, am, b4_words, b4_scales, b8_words, b8_s
         for q in range(4):
             load_b4_scales(q)
         load_b4(0)
-        load_b8_scales(0)
-        load_b8_scales(1)
         load_b8(0)
-        load_b8_scales(2)
-        load_b8_scales(3)
         load_b4(1)
         load_b8(1)
 
@@ -125,8 +123,8 @@ def tile_mix_kfac_res_none_kernel(tc, g, am, b4_words, b4_scales, b8_words, b8_s
         def round_g(engine, a, c, p0, p1):
             copy_on(
                 engine,
-                g_bf[a][:, :, G_CHUNKS[a, c][0] + p0 : G_CHUNKS[a, c][0] + p1, :].rearrange("p i s j -> p s j i"),
-                g_raw[a, c][:, :, PACK * p0 : PACK * p1].rearrange("p j (s i) -> p s j i", i=PACK),
+                g_bf[a][:, :, G_CHUNKS[a, c][0] + p0 : G_CHUNKS[a, c][0] + p1, :].rearrange("p i s j -> p s i j"),
+                g_raw[a, c][:, :, PACK * p0 : PACK * p1].rearrange("p j (s i) -> p s i j", i=PACK),
             )
 
         def round_g_chunk(a, c):

@@ -19,10 +19,9 @@ PACK = 4
 PASS = P * PACK
 BANK = 512
 AM_CHUNK = 256
-AM_V = 168
-G_CHUNKS = {(0, 0): (0, 64), (0, 1): (64, 128), (1, 0): (0, 64), (1, 1): (64, 128)}
-G_V = {(0, 0): 44, (0, 1): 44, (1, 0): 64, (1, 1): 64}
-WARM = ((256, 4), (512, 3))
+G_CHUNKS = {(0, 0): (0, 128), (1, 0): (0, 96), (1, 1): (96, 128)}
+G_V = {(0, 0): 86, (1, 0): 80, (1, 1): 32}
+WARM = ((256, 4), (512, 2))
 TAIL = ((0, 256, 7, "s"), (256, 128, 0, "v"), (384, 128, 1, "s"))
 
 
@@ -40,7 +39,7 @@ def tile_mix_kfac_res_none_kernel(tc, g, am, b4_words, b4_scales, b8_words, b8_s
         def bank(n, name):
             return ps.tile([P, BANK], F32, name=name, tag="bank%d" % n)
 
-        am_raw = [keep("am_raw%d" % c, [P, PACK, AM_CHUNK], F32) for c in range(2)]
+        am_raw = keep("am_raw", [P, PACK, M], F32)
         am_bf = keep("am_bf", [P, M, PACK], BF16)
         am_codes = keep("am_codes", [P, M], U32)
         am_scale = keep("am_scale", [P, M], U8)
@@ -85,11 +84,8 @@ def tile_mix_kfac_res_none_kernel(tc, g, am, b4_words, b4_scales, b8_words, b8_s
         for q in range(4):
             load_b8_scales(q)
         nc.vector.memset(b4_plane[:].rearrange("p a n -> p (a n)").bitcast(I32), 0)
-        am_k = am.rearrange("(p j) m -> p j m", j=PACK)
-        for c in range(2):
-            nc.sync.dma_start(out=am_raw[c][:], in_=am_k[:, :, c * AM_CHUNK : (c + 1) * AM_CHUNK])
+        nc.sync.dma_start(out=am_raw[:], in_=am.rearrange("(p j) m -> p j m", j=PACK))
         load_g(0, 0)
-        load_g(0, 1)
         load_g(1, 0)
         load_g(1, 1)
         for q in range(4):
@@ -105,11 +101,12 @@ def tile_mix_kfac_res_none_kernel(tc, g, am, b4_words, b4_scales, b8_words, b8_s
             else:
                 nc.scalar.copy(out=dst, in_=src)
 
-        def round_am(engine, c, m0, m1):
+        def round_am(engine, c):
+            cols = slice(c * AM_CHUNK, (c + 1) * AM_CHUNK)
             copy_on(
                 engine,
-                am_bf[:, c * AM_CHUNK + m0 : c * AM_CHUNK + m1, :].rearrange("p (c u) j -> p c j u", u=4),
-                am_raw[c][:, :, m0:m1].rearrange("p j (c u) -> p c j u", u=4),
+                am_bf[:, cols, :].rearrange("p (c u) j -> p c j u", u=4),
+                am_raw[:, :, cols].rearrange("p j (c u) -> p c j u", u=4),
             )
 
         def quantize_am(c):
@@ -225,8 +222,7 @@ def tile_mix_kfac_res_none_kernel(tc, g, am, b4_words, b4_scales, b8_words, b8_s
 
         warm = bank(7, "warm")
         for c in range(2):
-            round_am("v", c, 0, AM_V)
-            round_am("s", c, AM_V, AM_CHUNK)
+            round_am("vs"[c], c)
             quantize_am(c)
             width, count = WARM[c]
             for w in range(count):
@@ -240,7 +236,6 @@ def tile_mix_kfac_res_none_kernel(tc, g, am, b4_words, b4_scales, b8_words, b8_s
                     stop=True,
                 )
         round_g_chunk(0, 0)
-        round_g_chunk(0, 1)
         for i in range(4):
             quantize_g(0, i)
             h_pass(0, i)
@@ -256,25 +251,22 @@ def tile_mix_kfac_res_none_kernel(tc, g, am, b4_words, b4_scales, b8_words, b8_s
             weave_h("v", 0, t)
             quantize_h(0, t)
             open_y(t)
-        for i in range(3):
-            drain_h("s", 1, i)
-        weave_h("v", 0, 2)
-        drain_h("v", 1, 3)
-        quantize_h(0, 2)
-        open_y(2)
-        weave_h("v", 1, 0)
-        weave_h("v", 1, 1)
-        quantize_h(1, 0)
-        quantize_h(1, 1)
-        weave_h("v", 1, 2)
-        weave_h("v", 0, 3)
-        quantize_h(1, 2)
-        weave_h("v", 1, 3)
-        quantize_h(0, 3)
-        quantize_h(1, 3)
-        for t in range(3):
+        for i in range(4):
+            drain_h("s" if i < 3 else "v", 1, i, 0, 2 * P)
+        for i in range(4):
+            drain_h("s", 1, i, 2 * P, M)
+        for t in range(2):
+            weave_h("v", 1, t)
+            quantize_h(1, t)
             for half in range(2):
-                close_y("s" if (t, half) != (2, 0) else "v", t, half)
-        whole_y("s", 6, 3, 0, BANK)
+                close_y("s", t, half)
+        for t in range(2, 4):
+            weave_h("v", 0, t)
+            weave_h("v", 1, t)
+            quantize_h(0, t)
+            quantize_h(1, t)
+        whole_y("v", 4, 2, 0, BANK)
+        whole_y("s", 5, 2, BANK, BANK)
+        whole_y("v", 6, 3, 0, BANK)
         for c0, width, number, engine in TAIL:
             whole_y(engine, number, 3, BANK + c0, width)

@@ -21,7 +21,7 @@ BANK = 512
 AM_CHUNK = 256
 G_CHUNKS = {(0, 0): (0, 128), (1, 0): (0, 96), (1, 1): (96, 128)}
 G_V = {(0, 0): 86, (1, 0): 80, (1, 1): 32}
-WARM = ((256, 4), (512, 2))
+WARM = ((256, 3), (512, 2))
 TAIL = ((0, 256, 7, "s"), (256, 128, 0, "v"), (384, 128, 1, "s"))
 
 
@@ -64,8 +64,8 @@ def tile_mix_kfac_res_none_kernel(tc, g, am, b4_words, b4_scales, b8_words, b8_s
 
         def load_b4_scales(q):
             nc.sync.dma_start(
-                out=b4_plane[32 * q : 32 * q + 4, :, :].bitcast(I32),
-                in_=b4_scales[:, 4 * q : 4 * q + 4, :].rearrange("a r n -> r a n").bitcast(I32),
+                out=b4_plane[q:P:32, :, :].bitcast(I32),
+                in_=b4_scales[:, q:16:4, :].rearrange("a r n -> r a n").bitcast(I32),
             )
 
         def load_b8_scales(q):

@@ -21,7 +21,7 @@ BANK = 512
 AM_CHUNK = 256
 G_CHUNKS = {(0, 0): (0, 128), (1, 0): (0, 96), (1, 1): (96, 128)}
 G_V = {(0, 0): 86, (1, 0): 80, (1, 1): 32}
-WARM = ((256, 3), (512, 2))
+WARM = ((256, 2), (512, 2))
 TAIL = ((0, 256, 7, "s"), (256, 128, 0, "v"), (384, 128, 1, "s"))
 
 
@@ -29,7 +29,7 @@ def tile_mix_kfac_res_none_kernel(tc, g, am, b4_words, b4_scales, b8_words, b8_s
     nc = tc.nc
     with ExitStack() as ctx:
         sb = ctx.enter_context(tc.tile_pool(name="sb", bufs=1))
-        ys = ctx.enter_context(tc.tile_pool(name="ys", bufs=10))
+        ys = ctx.enter_context(tc.tile_pool(name="ys", bufs=12))
         ps = ctx.enter_context(tc.psum_pool(name="ps", bufs=1))
         ctx.enter_context(tc.manual_schedule())
 
@@ -210,7 +210,7 @@ def tile_mix_kfac_res_none_kernel(tc, g, am, b4_words, b4_scales, b8_words, b8_s
             b8_pass(y_banks[t, half][:], 1, t, half * BANK, BANK, False, True)
             store_y(engine, y_banks[t, half][:], t, half * BANK, BANK)
 
-        def whole_y(engine, number, t, n0, width):
+        def whole_y(engine, number, t, n0, width, pieces=1):
             acc = bank(number, "y%d_%d" % (t, n0))
             step = BANK if width == BANK else P
             b8_pass(acc[:, :width], 0, t, n0, width, True, False)
@@ -218,39 +218,48 @@ def tile_mix_kfac_res_none_kernel(tc, g, am, b4_words, b4_scales, b8_words, b8_s
                 for c0 in range(0, width, step):
                     b4_pass(acc[:, c0 : c0 + step], a, t, n0 + c0, step, False, False)
             b8_pass(acc[:, :width], 1, t, n0, width, False, True)
-            store_y(engine, acc[:, :width], t, n0, width)
+            for c0 in range(0, width, width // pieces):
+                store_y(engine, acc[:, c0 : c0 + width // pieces], t, n0 + c0, width // pieces)
 
         warm = bank(7, "warm")
+
+        def warm_up(width):
+            nc.tensor.matmul_mx(
+                out=warm[:, :width],
+                lhsT=am_codes[:, :P].bitcast(E4M3),
+                lhsT_scale=am_scale[:, :P],
+                rhs=am_codes[:, :width].bitcast(E4M3),
+                rhs_scale=am_scale[:, :width],
+                start=True,
+                stop=True,
+            )
+
         for c in range(2):
             round_am("vs"[c], c)
             quantize_am(c)
             width, count = WARM[c]
             for w in range(count):
-                nc.tensor.matmul_mx(
-                    out=warm[:, :width],
-                    lhsT=am_codes[:, :P].bitcast(E4M3),
-                    lhsT_scale=am_scale[:, :P],
-                    rhs=am_codes[:, :width].bitcast(E4M3),
-                    rhs_scale=am_scale[:, :width],
-                    start=True,
-                    stop=True,
-                )
+                warm_up(width)
         round_g_chunk(0, 0)
         for i in range(4):
             quantize_g(0, i)
             h_pass(0, i)
+        warm_up(BANK)
         round_g_chunk(1, 0)
         round_g_chunk(1, 1)
         for m0 in (0, 2 * P):
             for i in range(4):
                 drain_h("s", 0, i, m0, m0 + 2 * P)
         for i in range(4):
+            if i == 2:
+                weave_h("v", 0, 0)
             quantize_g(1, i)
             h_pass(1, i)
-        for t in range(2):
-            weave_h("v", 0, t)
-            quantize_h(0, t)
-            open_y(t)
+        quantize_h(0, 0)
+        open_y(0)
+        weave_h("v", 0, 1)
+        quantize_h(0, 1)
+        open_y(1)
         for i in range(4):
             drain_h("s" if i < 3 else "v", 1, i, 0, 2 * P)
         for i in range(4):
@@ -267,6 +276,6 @@ def tile_mix_kfac_res_none_kernel(tc, g, am, b4_words, b4_scales, b8_words, b8_s
             quantize_h(1, t)
         whole_y("v", 4, 2, 0, BANK)
         whole_y("s", 5, 2, BANK, BANK)
-        whole_y("v", 6, 3, 0, BANK)
+        whole_y("v", 6, 3, 0, BANK, 2)
         for c0, width, number, engine in TAIL:
             whole_y(engine, number, 3, BANK + c0, width)

@@ -197,8 +197,6 @@ def tile_mix_kfac_res_none_kernel(tc, g, am, b4_words, b4_scales, b8_words, b8_s
             for half in range(2):
                 y_banks[t, half] = bank(2 * t + half, "y%d%d" % (t, half))
                 b4_pass(y_banks[t, half][:], 0, t, half * BANK, BANK, True, False)
-            for half in range(2):
-                b8_pass(y_banks[t, half][:], 0, t, half * BANK, BANK, False, False)
 
         def store_y(engine, acc, t, n0, width):
             y = ys.tile([P, width], F32, name="y", tag="y")
@@ -206,7 +204,6 @@ def tile_mix_kfac_res_none_kernel(tc, g, am, b4_words, b4_scales, b8_words, b8_s
             nc.sync.dma_start(out=out[t * P : (t + 1) * P, n0 : n0 + width], in_=y[:])
 
         def close_y(engine, t, half):
-            b4_pass(y_banks[t, half][:], 1, t, half * BANK, BANK, False, False)
             b8_pass(y_banks[t, half][:], 1, t, half * BANK, BANK, False, True)
             store_y(engine, y_banks[t, half][:], t, half * BANK, BANK)
 
@@ -260,6 +257,9 @@ def tile_mix_kfac_res_none_kernel(tc, g, am, b4_words, b4_scales, b8_words, b8_s
         weave_h("v", 0, 1)
         quantize_h(0, 1)
         open_y(1)
+        for t in range(2):
+            for half in range(2):
+                b8_pass(y_banks[t, half][:], 0, t, half * BANK, BANK, False, False)
         for i in range(4):
             drain_h("s" if i < 3 else "v", 1, i, 0, 2 * P)
         for i in range(4):
@@ -267,6 +267,9 @@ def tile_mix_kfac_res_none_kernel(tc, g, am, b4_words, b4_scales, b8_words, b8_s
         for t in range(2):
             weave_h("v", 1, t)
             quantize_h(1, t)
+            for half in range(2):
+                b4_pass(y_banks[t, half][:], 1, t, half * BANK, BANK, False, False)
+        for t in range(2):
             for half in range(2):
                 close_y("s", t, half)
         for t in range(2, 4):

@@ -69,7 +69,7 @@ def tile_mix_kfac_res_none_kernel(tc, g, am, b4_words, b4_scales, b8_words, b8_s
             )
 
         def load_b8_scales(q):
-            nc.gpsimd.dma_start(
+            nc.sync.dma_start(
                 out=b8_plane[32 * q + 4 : 32 * q + 12, :].bitcast(I32),
                 in_=b8_scales[:, 4 * q : 4 * q + 4, :].bitcast(I32),
             )
@@ -80,10 +80,8 @@ def tile_mix_kfac_res_none_kernel(tc, g, am, b4_words, b4_scales, b8_words, b8_s
         def load_b8(a):
             nc.sync.dma_start(out=b8[a][:].bitcast(I32), in_=b8_words[a].rearrange("p n i -> p (n i)").bitcast(I32))
 
-        nc.gpsimd.memset(b8_plane[:].bitcast(I32), 0)
-        for q in range(4):
-            load_b8_scales(q)
         nc.vector.memset(b4_plane[:].rearrange("p a n -> p (a n)").bitcast(I32), 0)
+        nc.vector.memset(b8_plane[:].bitcast(I32), 0)
         nc.sync.dma_start(out=am_raw[:], in_=am.rearrange("(p j) m -> p j m", j=PACK))
         load_g(0, 0)
         load_g(1, 0)
@@ -92,6 +90,8 @@ def tile_mix_kfac_res_none_kernel(tc, g, am, b4_words, b4_scales, b8_words, b8_s
             load_b4_scales(q)
         load_b4(0)
         load_b8(0)
+        for q in range(4):
+            load_b8_scales(q)
         load_b4(1)
         load_b8(1)
 

@@ -53,7 +53,7 @@ def tile_mix_kfac_res_none_kernel(tc, g, am, b4_words, b4_scales, b8_words, b8_s
         h_scale = {(a, t): keep("h_scale%d%d" % (a, t), [P, P], U8) for a in range(2) for t in range(4)}
         b4 = [keep("b4_%d" % a, [P, 2 * N], U8) for a in range(2)]
         b8 = [keep("b8_%d" % a, [P, 4 * N], U8) for a in range(2)]
-        b4_plane = keep("b4_plane", [P, 2, N], U8)
+        b4_plane = [keep("b4_plane%d" % a, [P, N], U8) for a in range(2)]
         b8_plane = keep("b8_plane", [P, N], U8)
 
         g_k = g.rearrange("(p j) l -> p j l", j=PACK)
@@ -62,17 +62,16 @@ def tile_mix_kfac_res_none_kernel(tc, g, am, b4_words, b4_scales, b8_words, b8_s
             s0, s1 = G_CHUNKS[a, c]
             nc.sync.dma_start(out=g_raw[a, c][:], in_=g_k[:, :, a * PASS + PACK * s0 : a * PASS + PACK * s1])
 
-        def load_b4_scales(q):
-            nc.sync.dma_start(
-                out=b4_plane[q:P:32, :, :].bitcast(I32),
-                in_=b4_scales[:, q:16:4, :].rearrange("a r n -> r a n").bitcast(I32),
-            )
+        def load_b4_scales(a):
+            for r in range(4):
+                nc.sync.dma_start(out=b4_plane[a][r:P:32, :].bitcast(I32), in_=b4_scales[a, r:16:4, :].bitcast(I32))
 
-        def load_b8_scales(q):
-            nc.sync.dma_start(
-                out=b8_plane[32 * q + 4 : 32 * q + 12, :].bitcast(I32),
-                in_=b8_scales[:, 4 * q : 4 * q + 4, :].bitcast(I32),
-            )
+        def load_b8_scales():
+            for q in range(4):
+                nc.sync.dma_start(
+                    out=b8_plane[32 * q + 4 : 32 * q + 12, :].bitcast(I32),
+                    in_=b8_scales[:, 4 * q : 4 * q + 4, :].bitcast(I32),
+                )
 
         def load_b4(a):
             nc.sync.dma_start(out=b4[a][:].bitcast(I32), in_=b4_words[a].bitcast(I32))
@@ -80,20 +79,19 @@ def tile_mix_kfac_res_none_kernel(tc, g, am, b4_words, b4_scales, b8_words, b8_s
         def load_b8(a):
             nc.sync.dma_start(out=b8[a][:].bitcast(I32), in_=b8_words[a].rearrange("p n i -> p (n i)").bitcast(I32))
 
-        nc.vector.memset(b4_plane[:].rearrange("p a n -> p (a n)").bitcast(I32), 0)
-        nc.vector.memset(b8_plane[:].bitcast(I32), 0)
+        for plane in (b4_plane[0], b8_plane, b4_plane[1]):
+            nc.vector.memset(plane[:].bitcast(I32), 0)
         nc.sync.dma_start(out=am_raw[:], in_=am.rearrange("(p j) m -> p j m", j=PACK))
         load_g(0, 0)
         load_g(1, 0)
         load_g(1, 1)
-        for q in range(4):
-            load_b4_scales(q)
+        load_b4_scales(0)
         load_b4(0)
         load_b8(0)
-        for q in range(4):
-            load_b8_scales(q)
-        load_b4(1)
+        load_b8_scales()
         load_b8(1)
+        load_b4(1)
+        load_b4_scales(1)
 
         def copy_on(engine, dst, src):
             if engine == "v":
@@ -177,7 +175,7 @@ def tile_mix_kfac_res_none_kernel(tc, g, am, b4_words, b4_scales, b8_words, b8_s
                 lhsT=h_codes[a, t][:].bitcast(E4M3),
                 lhsT_scale=h_scale[a, t][:],
                 rhs=b4[a][:, 2 * n0 : 2 * (n0 + width)].bitcast(E2M1),
-                rhs_scale=b4_plane[:, a, n0 : n0 + width],
+                rhs_scale=b4_plane[a][:, n0 : n0 + width],
                 start=start,
                 stop=stop,
             )
@@ -204,7 +202,7 @@ def tile_mix_kfac_res_none_kernel(tc, g, am, b4_words, b4_scales, b8_words, b8_s
             nc.sync.dma_start(out=out[t * P : (t + 1) * P, n0 : n0 + width], in_=y[:])
 
         def close_y(engine, t, half):
-            b8_pass(y_banks[t, half][:], 1, t, half * BANK, BANK, False, True)
+            b4_pass(y_banks[t, half][:], 1, t, half * BANK, BANK, False, True)
             store_y(engine, y_banks[t, half][:], t, half * BANK, BANK)
 
         def whole_y(engine, number, t, n0, width, pieces=1):
@@ -268,7 +266,7 @@ def tile_mix_kfac_res_none_kernel(tc, g, am, b4_words, b4_scales, b8_words, b8_s
             weave_h("v", 1, t)
             quantize_h(1, t)
             for half in range(2):
-                b4_pass(y_banks[t, half][:], 1, t, half * BANK, BANK, False, False)
+                b8_pass(y_banks[t, half][:], 1, t, half * BANK, BANK, False, False)
         for t in range(2):
             for half in range(2):
                 close_y("s", t, half)

@@ -73,8 +73,10 @@ def tile_mix_kfac_res_none_kernel(tc, g, am, b4_words, b4_scales, b8_words, b8_s
                     in_=b8_scales[:, 4 * q : 4 * q + 4, :].bitcast(I32),
                 )
 
-        def load_b4(a):
-            nc.sync.dma_start(out=b4[a][:].bitcast(I32), in_=b4_words[a].bitcast(I32))
+        def load_b4(a, n0=0, n1=N):
+            nc.sync.dma_start(
+                out=b4[a][:, 2 * n0 : 2 * n1].bitcast(I32), in_=b4_words[a][:, 2 * n0 : 2 * n1].bitcast(I32)
+            )
 
         def load_b8(a):
             nc.sync.dma_start(out=b8[a][:].bitcast(I32), in_=b8_words[a].rearrange("p n i -> p (n i)").bitcast(I32))
@@ -90,8 +92,9 @@ def tile_mix_kfac_res_none_kernel(tc, g, am, b4_words, b4_scales, b8_words, b8_s
         load_b8(0)
         load_b8_scales()
         load_b8(1)
-        load_b4(1)
         load_b4_scales(1)
+        load_b4(1, 0, BANK)
+        load_b4(1, BANK, N)
 
         def copy_on(engine, dst, src):
             if engine == "v":
@@ -267,8 +270,8 @@ def tile_mix_kfac_res_none_kernel(tc, g, am, b4_words, b4_scales, b8_words, b8_s
             quantize_h(1, t)
             for half in range(2):
                 b8_pass(y_banks[t, half][:], 1, t, half * BANK, BANK, False, False)
-        for t in range(2):
-            for half in range(2):
+        for half in range(2):
+            for t in range(2):
                 close_y("s", t, half)
         for t in range(2, 4):
             weave_h("v", 0, t)

@@ -18,11 +18,11 @@ P = 128
 PACK = 4
 PASS = P * PACK
 BANK = 512
-AM_CHUNK = 256
 G_CHUNKS = {(0, 0): (0, 128), (1, 0): (0, 96), (1, 1): (96, 128)}
-G_V = {(0, 0): 86, (1, 0): 80, (1, 1): 32}
-WARM = ((256, 2), (512, 2))
-TAIL = ((0, 256, 7, "s"), (256, 128, 0, "v"), (384, 128, 1, "s"))
+G_V = {(0, 0): 86, (1, 1): 32}
+G_EARLY = 64
+WARM = (128, 256, 512)
+TAIL = ((0, 256, 0, "s"), (256, 256, 1, "v"), (512, 256, 2, "s"), (768, 128, 3, "v"), (896, 128, 6, "s"))
 
 
 def tile_mix_kfac_res_none_kernel(tc, g, am, b4_words, b4_scales, b8_words, b8_scales, out):
@@ -39,15 +39,14 @@ def tile_mix_kfac_res_none_kernel(tc, g, am, b4_words, b4_scales, b8_words, b8_s
         def bank(n, name):
             return ps.tile([P, BANK], F32, name=name, tag="bank%d" % n)
 
-        am_raw = keep("am_raw", [P, PACK, M], F32)
-        am_bf = keep("am_bf", [P, M, PACK], BF16)
-        am_codes = keep("am_codes", [P, M], U32)
-        am_scale = keep("am_scale", [P, M], U8)
+        am_raw = [keep("am_raw0", [P, PACK, 3 * P], F32), keep("am_raw1", [P, PACK, P], F32)]
+        am_bf = [keep("am_bf%d" % t, [P, P, PACK], BF16) for t in range(4)]
+        am_codes = [keep("am_codes%d" % t, [P, P], U32) for t in range(4)]
+        am_scale = [keep("am_scale%d" % t, [P, P], U8) for t in range(4)]
         g_raw = {key: keep("g_raw%d%d" % key, [P, PACK, PACK * (s1 - s0)], F32) for key, (s0, s1) in G_CHUNKS.items()}
         g_bf = [keep("g_bf%d" % a, [P, PACK, P, PACK], BF16) for a in range(2)]
         g_codes = [keep("g_codes%d" % a, [P, PACK, P], U32) for a in range(2)]
         g_scale = [keep("g_scale%d" % a, [P, PACK, P], U8) for a in range(2)]
-        h_rows = [keep("h_rows%d" % a, [P, PACK, M], BF16) for a in range(2)]
         h_bf = {(a, t): keep("h_bf%d%d" % (a, t), [P, P, PACK], BF16) for a in range(2) for t in range(4)}
         h_codes = {(a, t): keep("h_codes%d%d" % (a, t), [P, P], U32) for a in range(2) for t in range(4)}
         h_scale = {(a, t): keep("h_scale%d%d" % (a, t), [P, P], U8) for a in range(2) for t in range(4)}
@@ -83,15 +82,17 @@ def tile_mix_kfac_res_none_kernel(tc, g, am, b4_words, b4_scales, b8_words, b8_s
 
         for plane in (b4_plane[0], b8_plane, b4_plane[1]):
             nc.vector.memset(plane[:].bitcast(I32), 0)
-        nc.sync.dma_start(out=am_raw[:], in_=am.rearrange("(p j) m -> p j m", j=PACK))
+        am_k = am.rearrange("(p j) m -> p j m", j=PACK)
         load_g(0, 0)
+        nc.sync.dma_start(out=am_raw[0][:], in_=am_k[:, :, : 3 * P])
         load_g(1, 0)
-        load_g(1, 1)
         load_b4_scales(0)
         load_b4(0)
-        load_b8(0)
+        load_g(1, 1)
         load_b8_scales()
+        load_b8(0)
         load_b8(1)
+        nc.sync.dma_start(out=am_raw[1][:], in_=am_k[:, :, 3 * P :])
         load_b4_scales(1)
         load_b4(1, 0, BANK)
         load_b4(1, BANK, N)
@@ -102,20 +103,18 @@ def tile_mix_kfac_res_none_kernel(tc, g, am, b4_words, b4_scales, b8_words, b8_s
             else:
                 nc.scalar.copy(out=dst, in_=src)
 
-        def round_am(engine, c):
-            cols = slice(c * AM_CHUNK, (c + 1) * AM_CHUNK)
+        def round_am(engine, t):
             copy_on(
                 engine,
-                am_bf[:, cols, :].rearrange("p (c u) j -> p c j u", u=4),
-                am_raw[:, :, cols].rearrange("p j (c u) -> p c j u", u=4),
+                am_bf[t][:].rearrange("p (c u) j -> p c j u", u=4),
+                am_raw[t // 3][:, :, t % 3 * P : (t % 3 + 1) * P].rearrange("p j (c u) -> p c j u", u=4),
             )
 
-        def quantize_am(c):
-            cols = slice(c * AM_CHUNK, (c + 1) * AM_CHUNK)
+        def quantize_am(t):
             nc.vector.quantize_mx(
-                out=am_codes[:, cols].bitcast(E4M3),
-                scales=am_scale[:, cols],
-                in_=am_bf[:, cols, :].rearrange("p m j -> p (m j)"),
+                out=am_codes[t][:].bitcast(E4M3),
+                scales=am_scale[t][:],
+                in_=am_bf[t][:].rearrange("p m j -> p (m j)"),
             )
 
         def round_g(engine, a, c, p0, p1):
@@ -141,27 +140,21 @@ def tile_mix_kfac_res_none_kernel(tc, g, am, b4_words, b4_scales, b8_words, b8_s
 
         h_banks = {}
 
-        def h_pass(a, i):
-            h_banks[a, i] = bank(4 * a + i, "h%d%d" % (a, i))
-            nc.tensor.matmul_mx(
-                out=h_banks[a, i][:],
-                lhsT=g_codes[a][:, i, :].bitcast(E5M2),
-                lhsT_scale=g_scale[a][:, i, :],
-                rhs=am_codes[:].bitcast(E4M3),
-                rhs_scale=am_scale[:],
-                start=True,
-                stop=True,
-            )
+        def h_passes(a, t, number):
+            h_banks[a, t] = bank(number, "h%d%d" % (a, t))
+            for i in range(PACK):
+                nc.tensor.matmul_mx(
+                    out=h_banks[a, t][:, i * P : (i + 1) * P],
+                    lhsT=g_codes[a][:, i, :].bitcast(E5M2),
+                    lhsT_scale=g_scale[a][:, i, :],
+                    rhs=am_codes[t][:].bitcast(E4M3),
+                    rhs_scale=am_scale[t][:],
+                    start=True,
+                    stop=True,
+                )
 
-        def drain_h(engine, a, i, m0=0, m1=M):
-            copy_on(engine, h_rows[a][:, i, m0:m1], h_banks[a, i][:, m0:m1])
-
-        def weave_h(engine, a, t):
-            copy_on(
-                engine,
-                h_bf[a, t][:].rearrange("p (c u) i -> p c i u", u=4),
-                h_rows[a][:, :, t * P : (t + 1) * P].rearrange("p i (c u) -> p c i u", u=4),
-            )
+        def drain_h(engine, a, t):
+            copy_on(engine, h_bf[a, t][:], h_banks[a, t][:].rearrange("p (i m) -> p m i", i=PACK))
 
         def quantize_h(a, t):
             nc.vector.quantize_mx(
@@ -194,92 +187,100 @@ def tile_mix_kfac_res_none_kernel(tc, g, am, b4_words, b4_scales, b8_words, b8_s
                 stop=stop,
             )
 
-        def open_y(t):
-            for half in range(2):
-                y_banks[t, half] = bank(2 * t + half, "y%d%d" % (t, half))
-                b4_pass(y_banks[t, half][:], 0, t, half * BANK, BANK, True, False)
+        def open_y(t, half):
+            y_banks[t, half] = bank(2 * t + half, "y%d%d" % (t, half))
+            b4_pass(y_banks[t, half][:], 0, t, half * BANK, BANK, True, False)
+
+        def add_b8(t, half):
+            b8_pass(y_banks[t, half][:], 0, t, half * BANK, BANK, False, False)
+
+        def close_y(t, half):
+            b8_pass(y_banks[t, half][:], 1, t, half * BANK, BANK, False, False)
+            b4_pass(y_banks[t, half][:], 1, t, half * BANK, BANK, False, True)
 
         def store_y(engine, acc, t, n0, width):
             y = ys.tile([P, width], F32, name="y", tag="y")
             copy_on(engine, y[:], acc)
             nc.sync.dma_start(out=out[t * P : (t + 1) * P, n0 : n0 + width], in_=y[:])
 
-        def close_y(engine, t, half):
-            b4_pass(y_banks[t, half][:], 1, t, half * BANK, BANK, False, True)
+        def store_half(engine, t, half):
             store_y(engine, y_banks[t, half][:], t, half * BANK, BANK)
 
-        def whole_y(engine, number, t, n0, width, pieces=1):
+        def whole_y(engine, number, t, n0, width):
             acc = bank(number, "y%d_%d" % (t, n0))
-            step = BANK if width == BANK else P
             b8_pass(acc[:, :width], 0, t, n0, width, True, False)
-            for a in range(2):
-                for c0 in range(0, width, step):
-                    b4_pass(acc[:, c0 : c0 + step], a, t, n0 + c0, step, False, False)
+            b4_pass(acc[:, :width], 0, t, n0, width, False, False)
+            b4_pass(acc[:, :width], 1, t, n0, width, False, False)
             b8_pass(acc[:, :width], 1, t, n0, width, False, True)
-            for c0 in range(0, width, width // pieces):
-                store_y(engine, acc[:, c0 : c0 + width // pieces], t, n0 + c0, width // pieces)
+            store_y(engine, acc[:, :width], t, n0, width)
 
-        warm = bank(7, "warm")
+        warm = bank(0, "warm")
 
         def warm_up(width):
             nc.tensor.matmul_mx(
                 out=warm[:, :width],
-                lhsT=am_codes[:, :P].bitcast(E4M3),
-                lhsT_scale=am_scale[:, :P],
-                rhs=am_codes[:, :width].bitcast(E4M3),
-                rhs_scale=am_scale[:, :width],
+                lhsT=g_codes[0][:, 0, :].bitcast(E5M2),
+                lhsT_scale=g_scale[0][:, 0, :],
+                rhs=g_codes[0][:].rearrange("p i s -> p (i s)")[:, :width].bitcast(E4M3),
+                rhs_scale=g_scale[0][:].rearrange("p i s -> p (i s)")[:, :width],
                 start=True,
                 stop=True,
             )
 
-        for c in range(2):
-            round_am("vs"[c], c)
-            quantize_am(c)
-            width, count = WARM[c]
-            for w in range(count):
-                warm_up(width)
         round_g_chunk(0, 0)
-        for i in range(4):
+        for i in range(PACK):
             quantize_g(0, i)
-            h_pass(0, i)
-        warm_up(BANK)
-        round_g_chunk(1, 0)
-        round_g_chunk(1, 1)
-        for m0 in (0, 2 * P):
-            for i in range(4):
-                drain_h("s", 0, i, m0, m0 + 2 * P)
-        for i in range(4):
-            if i == 2:
-                weave_h("v", 0, 0)
-            quantize_g(1, i)
-            h_pass(1, i)
-        quantize_h(0, 0)
-        open_y(0)
-        weave_h("v", 0, 1)
-        quantize_h(0, 1)
-        open_y(1)
-        for t in range(2):
-            for half in range(2):
-                b8_pass(y_banks[t, half][:], 0, t, half * BANK, BANK, False, False)
-        for i in range(4):
-            drain_h("s" if i < 3 else "v", 1, i, 0, 2 * P)
-        for i in range(4):
-            drain_h("s", 1, i, 2 * P, M)
-        for t in range(2):
-            weave_h("v", 1, t)
-            quantize_h(1, t)
-            for half in range(2):
-                b8_pass(y_banks[t, half][:], 1, t, half * BANK, BANK, False, False)
-        for half in range(2):
-            for t in range(2):
-                close_y("s", t, half)
-        for t in range(2, 4):
-            weave_h("v", 0, t)
-            weave_h("v", 1, t)
+        for width in WARM:
+            warm_up(width)
+        round_am("v", 0)
+        round_am("s", 1)
+        round_am("v", 2)
+        for t in range(3):
+            quantize_am(t)
+            h_passes(0, t, 5 + t)
+        round_g("v", 1, 0, 0, G_EARLY)
+        for t in range(3):
+            drain_h("s", 0, t)
+            if t == 2:
+                round_g_chunk(1, 1)
             quantize_h(0, t)
+            if t == 0:
+                round_g("v", 1, 0, G_EARLY, G_CHUNKS[1, 0][1])
+            for half in range(2):
+                open_y(t, half)
+        for i in range(PACK):
+            quantize_g(1, i)
+        for t in range(2):
+            h_passes(1, t, 6 + t)
+            drain_h("s", 1, t)
             quantize_h(1, t)
-        whole_y("v", 4, 2, 0, BANK)
-        whole_y("s", 5, 2, BANK, BANK)
-        whole_y("v", 6, 3, 0, BANK, 2)
+        for t in range(2):
+            for half in range(2):
+                add_b8(t, half)
+        h_passes(1, 2, 6)
+        round_am("v", 3)
+        drain_h("s", 1, 2)
+        for half in range(2):
+            add_b8(2, half)
+        quantize_am(3)
+        quantize_h(1, 2)
+        close_y(0, 0)
+        h_passes(0, 3, 7)
+        drain_h("s", 0, 3)
+        store_half("v", 0, 0)
+        close_y(0, 1)
+        h_passes(1, 3, 6)
+        store_half("v", 0, 1)
+        drain_h("s", 1, 3)
+        quantize_h(0, 3)
+        close_y(1, 0)
+        store_half("s", 1, 0)
+        quantize_h(1, 3)
+        close_y(1, 1)
+        store_half("v", 1, 1)
+        close_y(2, 0)
+        store_half("s", 2, 0)
+        close_y(2, 1)
+        store_half("v", 2, 1)
         for c0, width, number, engine in TAIL:
-            whole_y(engine, number, 3, BANK + c0, width)
+            whole_y(engine, number, 3, c0, width)

@@ -21,7 +21,7 @@ BANK = 512
 G_CHUNKS = {(0, 0): (0, 128), (1, 0): (0, 96), (1, 1): (96, 128)}
 G_V = {(0, 0): 86, (1, 1): 32}
 G_EARLY = 64
-WARM = (128, 256, 512)
+WARM = (128, 256, 512, 256)
 TAIL = ((0, 256, 0, "s"), (256, 256, 1, "v"), (512, 256, 2, "s"), (768, 128, 3, "v"), (896, 128, 6, "s"))
 
 
@@ -39,7 +39,7 @@ def tile_mix_kfac_res_none_kernel(tc, g, am, b4_words, b4_scales, b8_words, b8_s
         def bank(n, name):
             return ps.tile([P, BANK], F32, name=name, tag="bank%d" % n)
 
-        am_raw = [keep("am_raw0", [P, PACK, 3 * P], F32), keep("am_raw1", [P, PACK, P], F32)]
+        am_raw = keep("am_raw", [P, PACK, M], F32)
         am_bf = [keep("am_bf%d" % t, [P, P, PACK], BF16) for t in range(4)]
         am_codes = [keep("am_codes%d" % t, [P, P], U32) for t in range(4)]
         am_scale = [keep("am_scale%d" % t, [P, P], U8) for t in range(4)]
@@ -52,7 +52,7 @@ def tile_mix_kfac_res_none_kernel(tc, g, am, b4_words, b4_scales, b8_words, b8_s
         h_scale = {(a, t): keep("h_scale%d%d" % (a, t), [P, P], U8) for a in range(2) for t in range(4)}
         b4 = [keep("b4_%d" % a, [P, 2 * N], U8) for a in range(2)]
         b8 = [keep("b8_%d" % a, [P, 4 * N], U8) for a in range(2)]
-        b4_plane = [keep("b4_plane%d" % a, [P, N], U8) for a in range(2)]
+        b4_plane = keep("b4_plane", [P, 2, N], U8)
         b8_plane = keep("b8_plane", [P, N], U8)
 
         g_k = g.rearrange("(p j) l -> p j l", j=PACK)
@@ -61,9 +61,12 @@ def tile_mix_kfac_res_none_kernel(tc, g, am, b4_words, b4_scales, b8_words, b8_s
             s0, s1 = G_CHUNKS[a, c]
             nc.sync.dma_start(out=g_raw[a, c][:], in_=g_k[:, :, a * PASS + PACK * s0 : a * PASS + PACK * s1])
 
-        def load_b4_scales(a):
+        def load_b4_scales():
             for r in range(4):
-                nc.sync.dma_start(out=b4_plane[a][r:P:32, :].bitcast(I32), in_=b4_scales[a, r:16:4, :].bitcast(I32))
+                nc.gpsimd.dma_start(
+                    out=b4_plane[r:P:32, :, :].bitcast(I32),
+                    in_=b4_scales[:, r:16:4, :].rearrange("a q n -> q a n").bitcast(I32),
+                )
 
         def load_b8_scales():
             for q in range(4):
@@ -80,22 +83,18 @@ def tile_mix_kfac_res_none_kernel(tc, g, am, b4_words, b4_scales, b8_words, b8_s
         def load_b8(a):
             nc.sync.dma_start(out=b8[a][:].bitcast(I32), in_=b8_words[a].rearrange("p n i -> p (n i)").bitcast(I32))
 
-        for plane in (b4_plane[0], b8_plane, b4_plane[1]):
+        for plane in (b4_plane, b8_plane):
             nc.vector.memset(plane[:].bitcast(I32), 0)
-        am_k = am.rearrange("(p j) m -> p j m", j=PACK)
+        load_b4_scales()
         load_g(0, 0)
-        nc.sync.dma_start(out=am_raw[0][:], in_=am_k[:, :, : 3 * P])
+        nc.sync.dma_start(out=am_raw[:], in_=am.rearrange("(p j) m -> p j m", j=PACK))
         load_g(1, 0)
-        load_b4_scales(0)
         load_b4(0)
         load_g(1, 1)
         load_b8_scales()
         load_b8(0)
         load_b8(1)
-        nc.sync.dma_start(out=am_raw[1][:], in_=am_k[:, :, 3 * P :])
-        load_b4_scales(1)
-        load_b4(1, 0, BANK)
-        load_b4(1, BANK, N)
+        load_b4(1)
 
         def copy_on(engine, dst, src):
             if engine == "v":
@@ -107,7 +106,7 @@ def tile_mix_kfac_res_none_kernel(tc, g, am, b4_words, b4_scales, b8_words, b8_s
             copy_on(
                 engine,
                 am_bf[t][:].rearrange("p (c u) j -> p c j u", u=4),
-                am_raw[t // 3][:, :, t % 3 * P : (t % 3 + 1) * P].rearrange("p j (c u) -> p c j u", u=4),
+                am_raw[:, :, t * P : (t + 1) * P].rearrange("p j (c u) -> p c j u", u=4),
             )
 
         def quantize_am(t):
@@ -171,7 +170,7 @@ def tile_mix_kfac_res_none_kernel(tc, g, am, b4_words, b4_scales, b8_words, b8_s
                 lhsT=h_codes[a, t][:].bitcast(E4M3),
                 lhsT_scale=h_scale[a, t][:],
                 rhs=b4[a][:, 2 * n0 : 2 * (n0 + width)].bitcast(E2M1),
-                rhs_scale=b4_plane[a][:, n0 : n0 + width],
+                rhs_scale=b4_plane[:, a, n0 : n0 + width],
                 start=start,
                 stop=stop,
             )
@@ -235,9 +234,11 @@ def tile_mix_kfac_res_none_kernel(tc, g, am, b4_words, b4_scales, b8_words, b8_s
         round_am("v", 0)
         round_am("s", 1)
         round_am("v", 2)
-        for t in range(3):
+        for t in range(4):
+            if t == 2:
+                round_am("v", 3)
             quantize_am(t)
-            h_passes(0, t, 5 + t)
+            h_passes(0, t, 4 + t)
         round_g("v", 1, 0, 0, G_EARLY)
         for t in range(3):
             drain_h("s", 0, t)
@@ -248,39 +249,33 @@ def tile_mix_kfac_res_none_kernel(tc, g, am, b4_words, b4_scales, b8_words, b8_s
                 round_g("v", 1, 0, G_EARLY, G_CHUNKS[1, 0][1])
             for half in range(2):
                 open_y(t, half)
+        drain_h("s", 0, 3)
         for i in range(PACK):
             quantize_g(1, i)
+        quantize_h(0, 3)
         for t in range(2):
             h_passes(1, t, 6 + t)
-            drain_h("s", 1, t)
+            drain_h("sv"[t], 1, t)
+        for t in range(2):
             quantize_h(1, t)
         for t in range(2):
             for half in range(2):
                 add_b8(t, half)
         h_passes(1, 2, 6)
-        round_am("v", 3)
         drain_h("s", 1, 2)
         for half in range(2):
-            add_b8(2, half)
-        quantize_am(3)
+            close_y(0, half)
+            store_half("vs"[half], 0, half)
         quantize_h(1, 2)
-        close_y(0, 0)
-        h_passes(0, 3, 7)
-        drain_h("s", 0, 3)
-        store_half("v", 0, 0)
-        close_y(0, 1)
-        h_passes(1, 3, 6)
-        store_half("v", 0, 1)
-        drain_h("s", 1, 3)
-        quantize_h(0, 3)
-        close_y(1, 0)
-        store_half("s", 1, 0)
+        h_passes(1, 3, 7)
+        drain_h("v", 1, 3)
+        for half in range(2):
+            close_y(1, half)
+            store_half("sv"[half], 1, half)
         quantize_h(1, 3)
-        close_y(1, 1)
-        store_half("v", 1, 1)
-        close_y(2, 0)
-        store_half("s", 2, 0)
-        close_y(2, 1)
-        store_half("v", 2, 1)
+        for half in range(2):
+            add_b8(2, half)
+            close_y(2, half)
+            store_half("sv"[half], 2, half)
         for c0, width, number, engine in TAIL:
             whole_y(engine, number, 3, c0, width)

@@ -139,21 +139,27 @@ def tile_mix_kfac_res_none_kernel(tc, g, am, b4_words, b4_scales, b8_words, b8_s
 
         h_banks = {}
 
-        def h_passes(a, t, number):
-            h_banks[a, t] = bank(number, "h%d%d" % (a, t))
+        def h_passes(a, tiles, number):
+            for n, t in enumerate(tiles):
+                h_banks[a, t] = bank(number + n, "h%d%d" % (a, t))
             for i in range(PACK):
-                nc.tensor.matmul_mx(
-                    out=h_banks[a, t][:, i * P : (i + 1) * P],
-                    lhsT=g_codes[a][:, i, :].bitcast(E5M2),
-                    lhsT_scale=g_scale[a][:, i, :],
-                    rhs=am_codes[t][:].bitcast(E4M3),
-                    rhs_scale=am_scale[t][:],
-                    start=True,
-                    stop=True,
-                )
+                for t in tiles:
+                    nc.tensor.matmul_mx(
+                        out=h_banks[a, t][:, i * P : (i + 1) * P],
+                        lhsT=g_codes[a][:, i, :].bitcast(E5M2),
+                        lhsT_scale=g_scale[a][:, i, :],
+                        rhs=am_codes[t][:].bitcast(E4M3),
+                        rhs_scale=am_scale[t][:],
+                        start=True,
+                        stop=True,
+                    )
 
         def drain_h(engine, a, t):
-            copy_on(engine, h_bf[a, t][:], h_banks[a, t][:].rearrange("p (i m) -> p m i", i=PACK))
+            copy_on(
+                engine,
+                h_bf[a, t][:].rearrange("p (c u) i -> p c i u", u=4),
+                h_banks[a, t][:].rearrange("p (i c u) -> p c i u", i=PACK, u=4),
+            )
 
         def quantize_h(a, t):
             nc.vector.quantize_mx(
@@ -238,7 +244,7 @@ def tile_mix_kfac_res_none_kernel(tc, g, am, b4_words, b4_scales, b8_words, b8_s
             if t == 2:
                 round_am("v", 3)
             quantize_am(t)
-            h_passes(0, t, 4 + t)
+            h_passes(0, [t], 4 + t)
         round_g("v", 1, 0, 0, G_EARLY)
         for t in range(3):
             drain_h("s", 0, t)
@@ -253,21 +259,21 @@ def tile_mix_kfac_res_none_kernel(tc, g, am, b4_words, b4_scales, b8_words, b8_s
         for i in range(PACK):
             quantize_g(1, i)
         quantize_h(0, 3)
+        h_passes(1, [0, 1], 6)
         for t in range(2):
-            h_passes(1, t, 6 + t)
             drain_h("sv"[t], 1, t)
         for t in range(2):
             quantize_h(1, t)
         for t in range(2):
             for half in range(2):
                 add_b8(t, half)
-        h_passes(1, 2, 6)
+        h_passes(1, [2], 6)
         drain_h("s", 1, 2)
         for half in range(2):
             close_y(0, half)
             store_half("vs"[half], 0, half)
         quantize_h(1, 2)
-        h_passes(1, 3, 7)
+        h_passes(1, [3], 7)
         drain_h("v", 1, 3)
         for half in range(2):
             close_y(1, half)

@@ -19,9 +19,10 @@ PACK = 4
 PASS = P * PACK
 BANK = 512
 G_CHUNKS = {(0, 0): (0, 128), (1, 0): (0, 96), (1, 1): (96, 128)}
-G_V = {(0, 0): 86, (1, 1): 32}
-G_EARLY = 64
-WARM = (128, 256, 512, 256)
+G_V = {(0, 0): 86, (1, 1): 14}
+G_EARLY = (0, 44, 76, 96)
+AM_V = 80
+WARM = (128, 128, 256, 512, 256)
 TAIL = ((0, 256, 0, "s"), (256, 256, 1, "v"), (512, 256, 2, "s"), (768, 128, 3, "v"), (896, 128, 6, "s"))
 
 
@@ -80,11 +81,14 @@ def tile_mix_kfac_res_none_kernel(tc, g, am, b4_words, b4_scales, b8_words, b8_s
                 out=b4[a][:, 2 * n0 : 2 * n1].bitcast(I32), in_=b4_words[a][:, 2 * n0 : 2 * n1].bitcast(I32)
             )
 
-        def load_b8(a):
-            nc.sync.dma_start(out=b8[a][:].bitcast(I32), in_=b8_words[a].rearrange("p n i -> p (n i)").bitcast(I32))
+        def load_b8(a, n0=0, n1=N):
+            nc.sync.dma_start(
+                out=b8[a][:, 4 * n0 : 4 * n1].bitcast(I32),
+                in_=b8_words[a].rearrange("p n i -> p (n i)")[:, 4 * n0 : 4 * n1].bitcast(I32),
+            )
 
-        for plane in (b4_plane, b8_plane):
-            nc.vector.memset(plane[:].bitcast(I32), 0)
+        nc.gpsimd.memset(b4_plane[:].bitcast(I32), 0)
+        nc.vector.memset(b8_plane[:].bitcast(I32), 0)
         load_b4_scales()
         load_g(0, 0)
         nc.sync.dma_start(out=am_raw[:], in_=am.rearrange("(p j) m -> p j m", j=PACK))
@@ -92,7 +96,8 @@ def tile_mix_kfac_res_none_kernel(tc, g, am, b4_words, b4_scales, b8_words, b8_s
         load_b4(0)
         load_g(1, 1)
         load_b8_scales()
-        load_b8(0)
+        load_b8(0, 0, BANK)
+        load_b8(0, BANK, N)
         load_b8(1)
         load_b4(1)
 
@@ -102,11 +107,11 @@ def tile_mix_kfac_res_none_kernel(tc, g, am, b4_words, b4_scales, b8_words, b8_s
             else:
                 nc.scalar.copy(out=dst, in_=src)
 
-        def round_am(engine, t):
+        def round_am(engine, t, m0=0, m1=P):
             copy_on(
                 engine,
-                am_bf[t][:].rearrange("p (c u) j -> p c j u", u=4),
-                am_raw[:, :, t * P : (t + 1) * P].rearrange("p j (c u) -> p c j u", u=4),
+                am_bf[t][:, m0:m1, :].rearrange("p (c u) j -> p c j u", u=4),
+                am_raw[:, :, t * P + m0 : t * P + m1].rearrange("p j (c u) -> p c j u", u=4),
             )
 
         def quantize_am(t):
@@ -237,22 +242,20 @@ def tile_mix_kfac_res_none_kernel(tc, g, am, b4_words, b4_scales, b8_words, b8_s
             quantize_g(0, i)
         for width in WARM:
             warm_up(width)
-        round_am("v", 0)
-        round_am("s", 1)
-        round_am("v", 2)
+        round_am("v", 0, 0, AM_V)
+        round_am("s", 0, AM_V, P)
+        round_am("s", 2)
         for t in range(4):
-            if t == 2:
-                round_am("v", 3)
+            if t % 2 == 0:
+                round_am("v", t + 1)
             quantize_am(t)
             h_passes(0, [t], 4 + t)
-        round_g("v", 1, 0, 0, G_EARLY)
         for t in range(3):
             drain_h("s", 0, t)
+            round_g("v", 1, 0, G_EARLY[t], G_EARLY[t + 1])
             if t == 2:
                 round_g_chunk(1, 1)
             quantize_h(0, t)
-            if t == 0:
-                round_g("v", 1, 0, G_EARLY, G_CHUNKS[1, 0][1])
             for half in range(2):
                 open_y(t, half)
         drain_h("s", 0, 3)
@@ -264,11 +267,12 @@ def tile_mix_kfac_res_none_kernel(tc, g, am, b4_words, b4_scales, b8_words, b8_s
             drain_h("sv"[t], 1, t)
         for t in range(2):
             quantize_h(1, t)
-        for t in range(2):
-            for half in range(2):
+        for half in range(2):
+            for t in range(2):
                 add_b8(t, half)
         h_passes(1, [2], 6)
         drain_h("s", 1, 2)
+        add_b8(2, 0)
         for half in range(2):
             close_y(0, half)
             store_half("vs"[half], 0, half)
@@ -280,7 +284,8 @@ def tile_mix_kfac_res_none_kernel(tc, g, am, b4_words, b4_scales, b8_words, b8_s
             store_half("sv"[half], 1, half)
         quantize_h(1, 3)
         for half in range(2):
-            add_b8(2, half)
+            if half:
+                add_b8(2, half)
             close_y(2, half)
             store_half("sv"[half], 2, half)
         for c0, width, number, engine in TAIL:

@@ -22,6 +22,7 @@ G_CHUNKS = {(0, 0): (0, 128), (1, 0): (0, 96), (1, 1): (96, 128)}
 G_V = {(0, 0): 86, (1, 1): 14}
 G_EARLY = (0, 44, 76, 96)
 AM_V = 80
+SHIFT = 16
 WARM = (128, 128, 256, 512, 256)
 TAIL = ((0, 256, 0, "s"), (256, 256, 1, "v"), (512, 256, 2, "s"), (768, 128, 3, "v"), (896, 128, 6, "s"))
 
@@ -35,7 +36,10 @@ def tile_mix_kfac_res_none_kernel(tc, g, am, b4_words, b4_scales, b8_words, b8_s
         ctx.enter_context(tc.manual_schedule())
 
         def keep(name, shape, dtype):
-            return sb.tile(shape, dtype, name=name, align_bytes=64)
+            return sb.tile(shape, dtype, name=name, align_bytes=256)
+
+        def keep_shifted(name, columns):
+            return keep(name, [P, SHIFT + columns], U32)[:, SHIFT:]
 
         def bank(n, name):
             return ps.tile([P, BANK], F32, name=name, tag="bank%d" % n)
@@ -46,10 +50,10 @@ def tile_mix_kfac_res_none_kernel(tc, g, am, b4_words, b4_scales, b8_words, b8_s
         am_scale = [keep("am_scale%d" % t, [P, P], U8) for t in range(4)]
         g_raw = {key: keep("g_raw%d%d" % key, [P, PACK, PACK * (s1 - s0)], F32) for key, (s0, s1) in G_CHUNKS.items()}
         g_bf = [keep("g_bf%d" % a, [P, PACK, P, PACK], BF16) for a in range(2)]
-        g_codes = [keep("g_codes%d" % a, [P, PACK, P], U32) for a in range(2)]
+        g_codes = [keep_shifted("g_codes%d" % a, PASS).rearrange("p (i s) -> p i s", i=PACK) for a in range(2)]
         g_scale = [keep("g_scale%d" % a, [P, PACK, P], U8) for a in range(2)]
         h_bf = {(a, t): keep("h_bf%d%d" % (a, t), [P, P, PACK], BF16) for a in range(2) for t in range(4)}
-        h_codes = {(a, t): keep("h_codes%d%d" % (a, t), [P, P], U32) for a in range(2) for t in range(4)}
+        h_codes = {(a, t): keep_shifted("h_codes%d%d" % (a, t), P) for a in range(2) for t in range(4)}
         h_scale = {(a, t): keep("h_scale%d%d" % (a, t), [P, P], U8) for a in range(2) for t in range(4)}
         b4 = [keep("b4_%d" % a, [P, 2 * N], U8) for a in range(2)]
         b8 = [keep("b8_%d" % a, [P, 4 * N], U8) for a in range(2)]
@@ -168,7 +172,7 @@ def tile_mix_kfac_res_none_kernel(tc, g, am, b4_words, b4_scales, b8_words, b8_s
 
         def quantize_h(a, t):
             nc.vector.quantize_mx(
-                out=h_codes[a, t][:].bitcast(E4M3),
+                out=h_codes[a, t].bitcast(E4M3),
                 scales=h_scale[a, t][:],
                 in_=h_bf[a, t][:].rearrange("p m i -> p (m i)"),
             )
@@ -178,7 +182,7 @@ def tile_mix_kfac_res_none_kernel(tc, g, am, b4_words, b4_scales, b8_words, b8_s
         def b4_pass(acc, a, t, n0, width, start, stop):
             nc.tensor.matmul_mx(
                 out=acc,
-                lhsT=h_codes[a, t][:].bitcast(E4M3),
+                lhsT=h_codes[a, t].bitcast(E4M3),
                 lhsT_scale=h_scale[a, t][:],
                 rhs=b4[a][:, 2 * n0 : 2 * (n0 + width)].bitcast(E2M1),
                 rhs_scale=b4_plane[:, a, n0 : n0 + width],
@@ -189,7 +193,7 @@ def tile_mix_kfac_res_none_kernel(tc, g, am, b4_words, b4_scales, b8_words, b8_s
         def b8_pass(acc, a, t, n0, width, start, stop):
             nc.tensor.matmul_mx(
                 out=acc,
-                lhsT=h_codes[a, t][:].bitcast(E4M3),
+                lhsT=h_codes[a, t].bitcast(E4M3),
                 lhsT_scale=h_scale[a, t][:],
                 rhs=b8[a][:, 4 * n0 : 4 * (n0 + width)].bitcast(E4M3),
                 rhs_scale=b8_plane[4 + 4 * a :, n0 : n0 + width],
@@ -231,7 +235,7 @@ def tile_mix_kfac_res_none_kernel(tc, g, am, b4_words, b4_scales, b8_words, b8_s
                 out=warm[:, :width],
                 lhsT=g_codes[0][:, 0, :].bitcast(E5M2),
                 lhsT_scale=g_scale[0][:, 0, :],
-                rhs=g_codes[0][:].rearrange("p i s -> p (i s)")[:, :width].bitcast(E4M3),
+                rhs=g_codes[0].rearrange("p i s -> p (i s)")[:, :width].bitcast(E4M3),
                 rhs_scale=g_scale[0][:].rearrange("p i s -> p (i s)")[:, :width],
                 start=True,
                 stop=True,

@@ -128,8 +128,8 @@ def tile_mix_kfac_res_none_kernel(tc, g, am, b4_words, b4_scales, b8_words, b8_s
         def round_g(engine, a, c, p0, p1):
             copy_on(
                 engine,
-                g_bf[a][:, :, G_CHUNKS[a, c][0] + p0 : G_CHUNKS[a, c][0] + p1, :].rearrange("p i s j -> p s i j"),
-                g_raw[a, c][:, :, PACK * p0 : PACK * p1].rearrange("p j (s i) -> p s i j", i=PACK),
+                g_bf[a][:, :, G_CHUNKS[a, c][0] + p0 : G_CHUNKS[a, c][0] + p1, :].rearrange("p i s (r j) -> p s r i j", r=2),
+                g_raw[a, c][:, :, PACK * p0 : PACK * p1].rearrange("p (r j) (s i) -> p s r i j", r=2, i=PACK),
             )
 
         def round_g_chunk(a, c):

@@ -55,7 +55,7 @@ def tile_mix_kfac_res_none_kernel(tc, g, am, b4_words, b4_scales, b8_words, b8_s
         h_bf = {(a, t): keep("h_bf%d%d" % (a, t), [P, P, PACK], BF16) for a in range(2) for t in range(4)}
         h_codes = {(a, t): keep_shifted("h_codes%d%d" % (a, t), P) for a in range(2) for t in range(4)}
         h_scale = {(a, t): keep("h_scale%d%d" % (a, t), [P, P], U8) for a in range(2) for t in range(4)}
-        b4 = [keep("b4_%d" % a, [P, 2 * N], U8) for a in range(2)]
+        b4 = [keep("b4_%d" % a, [P, 4 * SHIFT + 2 * N], U8)[:, 4 * SHIFT :] for a in range(2)]
         b8 = [keep("b8_%d" % a, [P, 4 * N], U8) for a in range(2)]
         b4_plane = keep("b4_plane", [P, 2, N], U8)
         b8_plane = keep("b8_plane", [P, N], U8)
@@ -213,7 +213,7 @@ def tile_mix_kfac_res_none_kernel(tc, g, am, b4_words, b4_scales, b8_words, b8_s
             b4_pass(y_banks[t, half][:], 1, t, half * BANK, BANK, False, True)
 
         def store_y(engine, acc, t, n0, width):
-            y = ys.tile([P, width], F32, name="y", tag="y")
+            y = ys.tile([P, width], F32, name="y", tag="y", align_bytes=256)
             copy_on(engine, y[:], acc)
             nc.sync.dma_start(out=out[t * P : (t + 1) * P, n0 : n0 + width], in_=y[:])
 

@@ -128,8 +128,8 @@ def tile_mix_kfac_res_none_kernel(tc, g, am, b4_words, b4_scales, b8_words, b8_s
         def round_g(engine, a, c, p0, p1):
             copy_on(
                 engine,
-                g_bf[a][:, :, G_CHUNKS[a, c][0] + p0 : G_CHUNKS[a, c][0] + p1, :].rearrange("p i s (r j) -> p s r i j", r=2),
-                g_raw[a, c][:, :, PACK * p0 : PACK * p1].rearrange("p (r j) (s i) -> p s r i j", r=2, i=PACK),
+                g_bf[a][:, :, G_CHUNKS[a, c][0] + p0 : G_CHUNKS[a, c][0] + p1, :].rearrange("p i s j -> p s j i"),
+                g_raw[a, c][:, :, PACK * p0 : PACK * p1].rearrange("p j (s i) -> p s j i", i=PACK),
             )
 
         def round_g_chunk(a, c):

from contextlib import ExitStack

import concourse.mybir as mybir

K, L, M, N = 512, 1024, 512, 1024
FLOPS = 2 * K * L * M + 2 * 2 * L * M * N

F32 = mybir.dt.float32
BF16 = mybir.dt.bfloat16
I32 = mybir.dt.int32
U32 = mybir.dt.uint32
U8 = mybir.dt.uint8
E4M3 = mybir.dt.float8_e4m3fn_x4
E5M2 = mybir.dt.float8_e5m2_x4
E2M1 = mybir.dt.float4_e2m1fn_x4

P = 128
PACK = 4
PASS = P * PACK
BANK = 512
G_CHUNKS = {(0, 0): (0, 128), (1, 0): (0, 96), (1, 1): (96, 128)}
G_V = {(0, 0): 86, (1, 1): 14}
G_EARLY = (0, 44, 76, 96)
AM_V = 80
SHIFT = 16
WARM = (128, 128, 256, 512, 256)
TAIL = ((0, 256, 0, "s"), (256, 256, 1, "v"), (512, 256, 2, "s"), (768, 128, 3, "v"), (896, 128, 6, "s"))


def tile_mix_kfac_res_none_kernel(tc, g, am, b4_words, b4_scales, b8_words, b8_scales, out):
    nc = tc.nc
    with ExitStack() as ctx:
        sb = ctx.enter_context(tc.tile_pool(name="sb", bufs=1))
        ys = ctx.enter_context(tc.tile_pool(name="ys", bufs=12))
        ps = ctx.enter_context(tc.psum_pool(name="ps", bufs=1))
        ctx.enter_context(tc.manual_schedule())

        def keep(name, shape, dtype):
            return sb.tile(shape, dtype, name=name, align_bytes=256)

        def keep_shifted(name, columns):
            return keep(name, [P, SHIFT + columns], U32)[:, SHIFT:]

        def bank(n, name):
            return ps.tile([P, BANK], F32, name=name, tag="bank%d" % n)

        am_raw = keep("am_raw", [P, PACK, M], F32)
        am_bf = [keep("am_bf%d" % t, [P, P, PACK], BF16) for t in range(4)]
        am_codes = [keep("am_codes%d" % t, [P, P], U32) for t in range(4)]
        am_scale = [keep("am_scale%d" % t, [P, P], U8) for t in range(4)]
        g_raw = {key: keep("g_raw%d%d" % key, [P, PACK, PACK * (s1 - s0)], F32) for key, (s0, s1) in G_CHUNKS.items()}
        g_bf = [keep("g_bf%d" % a, [P, PACK, P, PACK], BF16) for a in range(2)]
        g_codes = [keep_shifted("g_codes%d" % a, PASS).rearrange("p (i s) -> p i s", i=PACK) for a in range(2)]
        g_scale = [keep("g_scale%d" % a, [P, PACK, P], U8) for a in range(2)]
        h_bf = {(a, t): keep("h_bf%d%d" % (a, t), [P, P, PACK], BF16) for a in range(2) for t in range(4)}
        h_codes = {(a, t): keep_shifted("h_codes%d%d" % (a, t), P) for a in range(2) for t in range(4)}
        h_scale = {(a, t): keep("h_scale%d%d" % (a, t), [P, P], U8) for a in range(2) for t in range(4)}
        b4 = [keep("b4_%d" % a, [P, 4 * SHIFT + 2 * N], U8)[:, 4 * SHIFT :] for a in range(2)]
        b8 = [keep("b8_%d" % a, [P, 4 * N], U8) for a in range(2)]
        b4_plane = keep("b4_plane", [P, 2, N], U8)
        b8_plane = keep("b8_plane", [P, N], U8)

        g_k = g.rearrange("(p j) l -> p j l", j=PACK)

        def load_g(a, c):
            s0, s1 = G_CHUNKS[a, c]
            nc.sync.dma_start(out=g_raw[a, c][:], in_=g_k[:, :, a * PASS + PACK * s0 : a * PASS + PACK * s1])

        def load_b4_scales():
            for r in range(4):
                nc.gpsimd.dma_start(
                    out=b4_plane[r:P:32, :, :].bitcast(I32),
                    in_=b4_scales[:, r:16:4, :].rearrange("a q n -> q a n").bitcast(I32),
                )

        def load_b8_scales():
            for q in range(4):
                nc.sync.dma_start(
                    out=b8_plane[32 * q + 4 : 32 * q + 12, :].bitcast(I32),
                    in_=b8_scales[:, 4 * q : 4 * q + 4, :].bitcast(I32),
                )

        def load_b4(a, n0=0, n1=N):
            nc.sync.dma_start(
                out=b4[a][:, 2 * n0 : 2 * n1].bitcast(I32), in_=b4_words[a][:, 2 * n0 : 2 * n1].bitcast(I32)
            )

        def load_b8(a, n0=0, n1=N):
            nc.sync.dma_start(
                out=b8[a][:, 4 * n0 : 4 * n1].bitcast(I32),
                in_=b8_words[a].rearrange("p n i -> p (n i)")[:, 4 * n0 : 4 * n1].bitcast(I32),
            )

        nc.gpsimd.memset(b4_plane[:].bitcast(I32), 0)
        nc.vector.memset(b8_plane[:].bitcast(I32), 0)
        load_b4_scales()
        load_g(0, 0)
        nc.sync.dma_start(out=am_raw[:], in_=am.rearrange("(p j) m -> p j m", j=PACK))
        load_g(1, 0)
        load_b4(0)
        load_g(1, 1)
        load_b8_scales()
        load_b8(0, 0, BANK)
        load_b8(0, BANK, N)
        load_b8(1)
        load_b4(1)

        def copy_on(engine, dst, src):
            if engine == "v":
                nc.vector.tensor_copy(out=dst, in_=src)
            else:
                nc.scalar.copy(out=dst, in_=src)

        def round_am(engine, t, m0=0, m1=P):
            copy_on(
                engine,
                am_bf[t][:, m0:m1, :].rearrange("p (c u) j -> p c j u", u=4),
                am_raw[:, :, t * P + m0 : t * P + m1].rearrange("p j (c u) -> p c j u", u=4),
            )

        def quantize_am(t):
            nc.vector.quantize_mx(
                out=am_codes[t][:].bitcast(E4M3),
                scales=am_scale[t][:],
                in_=am_bf[t][:].rearrange("p m j -> p (m j)"),
            )

        def round_g(engine, a, c, p0, p1):
            copy_on(
                engine,
                g_bf[a][:, :, G_CHUNKS[a, c][0] + p0 : G_CHUNKS[a, c][0] + p1, :].rearrange("p i s j -> p s j i"),
                g_raw[a, c][:, :, PACK * p0 : PACK * p1].rearrange("p j (s i) -> p s j i", i=PACK),
            )

        def round_g_chunk(a, c):
            split = G_V[a, c]
            round_g("v", a, c, 0, split)
            width = G_CHUNKS[a, c][1] - G_CHUNKS[a, c][0]
            if split < width:
                round_g("s", a, c, split, width)

        def quantize_g(a, i):
            nc.vector.quantize_mx(
                out=g_codes[a][:, i, :].bitcast(E5M2),
                scales=g_scale[a][:, i, :],
                in_=g_bf[a][:, i, :, :].rearrange("p s j -> p (s j)"),
            )

        h_banks = {}

        def h_passes(a, tiles, number):
            for n, t in enumerate(tiles):
                h_banks[a, t] = bank(number + n, "h%d%d" % (a, t))
            for i in range(PACK):
                for t in tiles:
                    nc.tensor.matmul_mx(
                        out=h_banks[a, t][:, i * P : (i + 1) * P],
                        lhsT=g_codes[a][:, i, :].bitcast(E5M2),
                        lhsT_scale=g_scale[a][:, i, :],
                        rhs=am_codes[t][:].bitcast(E4M3),
                        rhs_scale=am_scale[t][:],
                        start=True,
                        stop=True,
                    )

        def drain_h(engine, a, t):
            copy_on(
                engine,
                h_bf[a, t][:].rearrange("p (c u) i -> p c i u", u=4),
                h_banks[a, t][:].rearrange("p (i c u) -> p c i u", i=PACK, u=4),
            )

        def quantize_h(a, t):
            nc.vector.quantize_mx(
                out=h_codes[a, t].bitcast(E4M3),
                scales=h_scale[a, t][:],
                in_=h_bf[a, t][:].rearrange("p m i -> p (m i)"),
            )

        y_banks = {}

        def b4_pass(acc, a, t, n0, width, start, stop):
            nc.tensor.matmul_mx(
                out=acc,
                lhsT=h_codes[a, t].bitcast(E4M3),
                lhsT_scale=h_scale[a, t][:],
                rhs=b4[a][:, 2 * n0 : 2 * (n0 + width)].bitcast(E2M1),
                rhs_scale=b4_plane[:, a, n0 : n0 + width],
                start=start,
                stop=stop,
            )

        def b8_pass(acc, a, t, n0, width, start, stop):
            nc.tensor.matmul_mx(
                out=acc,
                lhsT=h_codes[a, t].bitcast(E4M3),
                lhsT_scale=h_scale[a, t][:],
                rhs=b8[a][:, 4 * n0 : 4 * (n0 + width)].bitcast(E4M3),
                rhs_scale=b8_plane[4 + 4 * a :, n0 : n0 + width],
                start=start,
                stop=stop,
            )

        def open_y(t, half):
            y_banks[t, half] = bank(2 * t + half, "y%d%d" % (t, half))
            b4_pass(y_banks[t, half][:], 0, t, half * BANK, BANK, True, False)

        def add_b8(t, half):
            b8_pass(y_banks[t, half][:], 0, t, half * BANK, BANK, False, False)

        def close_y(t, half):
            b8_pass(y_banks[t, half][:], 1, t, half * BANK, BANK, False, False)
            b4_pass(y_banks[t, half][:], 1, t, half * BANK, BANK, False, True)

        def store_y(engine, acc, t, n0, width):
            y = ys.tile([P, width], F32, name="y", tag="y", align_bytes=256)
            copy_on(engine, y[:], acc)
            nc.sync.dma_start(out=out[t * P : (t + 1) * P, n0 : n0 + width], in_=y[:])

        def store_half(engine, t, half):
            store_y(engine, y_banks[t, half][:], t, half * BANK, BANK)

        def whole_y(engine, number, t, n0, width):
            acc = bank(number, "y%d_%d" % (t, n0))
            b8_pass(acc[:, :width], 0, t, n0, width, True, False)
            b4_pass(acc[:, :width], 0, t, n0, width, False, False)
            b4_pass(acc[:, :width], 1, t, n0, width, False, False)
            b8_pass(acc[:, :width], 1, t, n0, width, False, True)
            store_y(engine, acc[:, :width], t, n0, width)

        warm = bank(0, "warm")

        def warm_up(width):
            nc.tensor.matmul_mx(
                out=warm[:, :width],
                lhsT=g_codes[0][:, 0, :].bitcast(E5M2),
                lhsT_scale=g_scale[0][:, 0, :],
                rhs=g_codes[0].rearrange("p i s -> p (i s)")[:, :width].bitcast(E4M3),
                rhs_scale=g_scale[0][:].rearrange("p i s -> p (i s)")[:, :width],
                start=True,
                stop=True,
            )

        round_g_chunk(0, 0)
        for i in range(PACK):
            quantize_g(0, i)
        for width in WARM:
            warm_up(width)
        round_am("v", 0, 0, AM_V)
        round_am("s", 0, AM_V, P)
        round_am("s", 2)
        for t in range(4):
            if t % 2 == 0:
                round_am("v", t + 1)
            quantize_am(t)
            h_passes(0, [t], 4 + t)
        for t in range(3):
            drain_h("s", 0, t)
            round_g("v", 1, 0, G_EARLY[t], G_EARLY[t + 1])
            if t == 2:
                round_g_chunk(1, 1)
            quantize_h(0, t)
            for half in range(2):
                open_y(t, half)
        drain_h("s", 0, 3)
        for i in range(PACK):
            quantize_g(1, i)
        quantize_h(0, 3)
        h_passes(1, [0, 1], 6)
        for t in range(2):
            drain_h("sv"[t], 1, t)
        for t in range(2):
            quantize_h(1, t)
        for half in range(2):
            for t in range(2):
                add_b8(t, half)
        h_passes(1, [2], 6)
        drain_h("s", 1, 2)
        add_b8(2, 0)
        for half in range(2):
            close_y(0, half)
            store_half("vs"[half], 0, half)
        quantize_h(1, 2)
        h_passes(1, [3], 7)
        drain_h("v", 1, 3)
        for half in range(2):
            close_y(1, half)
            store_half("sv"[half], 1, half)
        quantize_h(1, 3)
        for half in range(2):
            if half:
                add_b8(2, half)
            close_y(2, half)
            store_half("sv"[half], 2, half)
        for c0, width, number, engine in TAIL:
            whole_y(engine, number, 3, c0, width)
